import numpy as np
import ml_dtypes


def mxq(x, axis, fmt="e4m3"):
    dtype, down = {"e4m3": (ml_dtypes.float8_e4m3fn, 7), "e5m2": (ml_dtypes.float8_e5m2, 14)}[fmt]
    v = np.moveaxis(np.asarray(x, np.float32).astype(ml_dtypes.bfloat16).astype(np.float64), axis, -1)
    blocks = v.reshape(v.shape[:-1] + (-1, 32))
    amax = np.abs(blocks).max(-1, keepdims=True)
    byte = np.maximum(np.where(amax > 0, np.frexp(amax)[1] - 1 + 127, 0) - down, 1)
    scale = np.exp2(byte - 127.0)
    codes = (blocks / scale).astype(np.float32).astype(dtype).astype(np.float64)
    return np.moveaxis((codes * scale).reshape(v.shape), -1, axis)


WIDE = False


def mx_kscale(k):
    if not WIDE:
        return np.ones(k)
    levels = np.array([10, -10, 5, -5, 0])
    if k % 512:
        return np.exp2(np.random.permutation(np.resize(levels, k // 32))).repeat(32)
    a = np.empty((k // 512, 16))
    for p in range(k // 512):
        a[p, :8] = np.random.permutation(np.resize(levels, 8))
        for g in range(8):
            far = levels[np.abs(levels - a[p, g]) >= 10]
            a[p, g + 8] = far[np.random.randint(len(far))]
    return np.exp2(a.ravel()).repeat(32)


def f64(x):
    return np.asarray(x).astype(np.float64)


def striped(idx):
    return np.tile(idx.reshape(-1, 16).T, (8, 1)).astype(np.uint16)


def unstriped(offs):
    return offs[:16].T.reshape(-1).astype(np.int64)


E2M1 = np.array([0.0, 0.5, 1.0, 1.5, 2.0, 3.0, 4.0, 6.0, -0.0, -0.5, -1.0, -1.5, -2.0, -3.0, -4.0, -6.0])


def pack_weight(w, fmt):
    k, n = w.shape
    w = f64(np.asarray(w, np.float32).astype(ml_dtypes.bfloat16)).reshape(k // 32, 32, n)
    amax = np.abs(w).max(1)
    if fmt == "e4m3":
        byte = np.frexp(amax)[1] - 1 + 127 - 7
    else:
        mant, ex = np.frexp(amax / 6.0)
        byte = np.where(mant > 0.5, ex, ex - 1) + 127
    byte = np.clip(np.where(amax > 0, byte, 1), 1, 254)
    scaled = (w * np.exp2(127.0 - byte)[:, None, :]).reshape(k, n).astype(np.float32)
    by_word = np.ascontiguousarray(scaled.reshape(k // 512, 128, 4, n).transpose(0, 1, 3, 2))
    if fmt == "e4m3":
        words = by_word.astype(ml_dtypes.float8_e4m3fn).view(np.uint8)
    else:
        c = by_word.astype(ml_dtypes.float4_e2m1fn).view(np.uint8) & 0xF
        words = (c[..., 0::2] | (c[..., 1::2] << 4)).reshape(k // 512, 128, 2 * n)
    return np.ascontiguousarray(words), np.ascontiguousarray(byte.astype(np.uint8).reshape(k // 512, 16, n))


def unpack_weight(words, scales, fmt):
    g, _, n = scales.shape
    words = np.ascontiguousarray(words).reshape(g, 128, n, -1)
    if fmt == "e4m3":
        vals = words.view(ml_dtypes.float8_e4m3fn).astype(np.float64)
    else:
        nib = np.empty((g, 128, n, 4), np.uint8)
        nib[..., 0::2] = words & 0xF
        nib[..., 1::2] = words >> 4
        vals = E2M1[nib]
    vals = vals * np.repeat(np.exp2(scales.astype(np.float64) - 127.0), 8, axis=1)[..., None]
    return vals.transpose(0, 1, 3, 2).reshape(g * 512, n)


def gelu(v):
    return 0.5 * v * (1.0 + np.tanh(np.sqrt(2.0 / np.pi) * (v + 0.044715 * v**3)))


K, T, K2, T2, S, P, H, N = 512, 2048, 1024, 2048, 1024, 1024, 512, 256

def setup_inputs():
    n = np.random.standard_normal
    s = mx_kscale(K)[:, None]
    s2 = mx_kscale(K2)[:, None]
    u = mx_kscale(H)[:, None]
    tab_words, tab_scales = pack_weight(n((K, T)) * s, "e4m3")
    wsc_words, wsc_scales = pack_weight(n((K, H)) / s / np.sqrt(K), "e2m1")
    wo_words, wo_scales = pack_weight(n((H, N)) / u / np.sqrt(H), "e4m3")
    return {
        "tab_words": tab_words, "tab_scales": tab_scales,
        "offs": striped(np.random.permutation(T)[:P]),
        "offs2": striped(np.random.permutation(T2)[:S]),
        "offs3": striped(np.random.permutation(T2)[:P]),
        "xs": (np.round(16 * n((K2, S))) / 16 * s2).astype(np.float32),
        "base": (n((K2, T2)) * s2).astype(np.float32),
        "wp": (n((K2, H)) / s2 * u.T / np.sqrt(K2)).astype(np.float32),
        "wsc_words": wsc_words, "wsc_scales": wsc_scales,
        "wsh": (n((K, H)) / s * u.T / np.sqrt(K)).astype(np.float32),
        "amp": np.random.uniform(0.15, 0.4, H).astype(np.float32),
        "wo_words": wo_words, "wo_scales": wo_scales,
        "bo": (0.5 * n(N)).astype(np.float32),
    }

def reference(tab_words, tab_scales, offs, offs2, offs3, xs, base, wp, wsc_words, wsc_scales, wsh, amp, wo_words, wo_scales, bo):
    page = f64(base).copy()
    page[:, unstriped(offs2)] = f64(xs)
    a = mxq(f64(wp), 0, "e4m3").T @ mxq(page, 0, "e4m3")
    x = a[:, unstriped(offs3)]
    v = unpack_weight(tab_words, tab_scales, "e4m3")[:, unstriped(offs)]
    sc = unpack_weight(wsc_words, wsc_scales, "e2m1").T @ v
    sh = mxq(f64(wsh), 0, "e4m3").T @ v
    z = x * np.exp(f64(amp)[:, None] * sc) + sh
    y = unpack_weight(wo_words, wo_scales, "e4m3").T @ mxq(z, 0, "e4m3")
    return y + f64(bo)[:, None]

@@ -1,0 +1,261 @@
+from contextlib import ExitStack
+
+import concourse.mybir as mybir
+
+F32 = mybir.dt.float32
+BF16 = mybir.dt.bfloat16
+I32 = mybir.dt.int32
+U32 = mybir.dt.uint32
+U16 = mybir.dt.uint16
+U8 = mybir.dt.uint8
+FP8X4 = mybir.dt.float8_e4m3fn_x4
+FP4X4 = mybir.dt.float4_e2m1fn_x4
+ACT = mybir.ActivationFunctionType
+ALU = mybir.AluOpType
+
+FLOPS = 3489660928
+
+P = 128
+PACK = 4
+T = 2048
+S = 1024
+H = 512
+BANK = 512
+HALF = 1024
+AL = 64
+LAST_SPLIT = 768
+
+
+def tile_list_tidal_pitch_features_kernel(tc, tab_words, tab_scales, offs, offs2, offs3, xs, base, wp,
+                                                    wsc_words, wsc_scales, wsh, amp, wo_words, wo_scales, bo, out):
+    nc = tc.nc
+    with ExitStack() as ctx:
+        lists = ctx.enter_context(tc.tile_pool(name="lists", bufs=1))
+        sb = ctx.enter_context(tc.tile_pool(name="sb", bufs=1))
+        psum = ctx.enter_context(tc.psum_pool(name="psum", bufs=1))
+
+        def sbuf(shape, dtype, name, tag=None):
+            return sb.tile(shape, dtype, name=name, tag=tag or name, align_bytes=AL)
+
+        def bank(b, shape, name):
+            return psum.tile(shape, F32, name=name, tag="bank%d" % b)
+
+        def load_scale_rows(queue, plane, rows):
+            for q in range(4):
+                queue.dma_start(out=plane[32 * q : 32 * q + 4, :].bitcast(I32), in_=rows[4 * q : 4 * q + 4, :].bitcast(I32))
+
+        base_rows = base.rearrange("(a p j) t -> a j p t", p=P, j=PACK)
+        xs_rows = xs.rearrange("(a p j) t -> a j p t", p=P, j=PACK)
+        planes = [sbuf([P, T], F32, "plane%d" % k) for k in range(8)]
+        fresh = [sbuf([P, S], F32, "fresh%d" % k) for k in range(7)]
+        fresh_last = [sbuf([P, LAST_SPLIT], F32, "fresh7a"), sbuf([P, S - LAST_SPLIT], F32, "fresh7b")]
+
+        def load_plane(k, pieces=1):
+            nc.sync.dma_start(out=planes[k][:], in_=base_rows[k // PACK, k % PACK])
+            w = S // pieces
+            for i in range(pieces):
+                nc.sync.dma_start(out=fresh[k][:, i * w : (i + 1) * w], in_=xs_rows[k // PACK, k % PACK][:, i * w : (i + 1) * w])
+
+        def scatter(k, pieces=1):
+            w = S // pieces
+            for i in range(pieces):
+                nc.vector.tensor_copy(out=planes[k][:].indirect(idx2[:, i * w // 16 : (i + 1) * w // 16]),
+                                      in_=fresh[k][:, i * w : (i + 1) * w])
+
+        def load_weight(rows, name, tag):
+            raw = sbuf([P, PACK, H], F32, name, tag)
+            nc.sync.dma_start(out=raw[:], in_=rows.rearrange("(p j) r -> p j r", j=PACK))
+            return raw
+
+        def weave_weight(raw, name):
+            woven = sbuf([P, H * PACK], BF16, name)
+            nc.scalar.copy(out=woven[:].rearrange("p (t m j) -> p m j t", t=PACK, j=PACK),
+                           in_=raw[:].rearrange("p j (m t) -> p m j t", t=PACK))
+            return woven
+
+        def quantize(codes, scales, woven):
+            nc.vector.quantize_mx(out=codes.bitcast(FP8X4), scales=scales, in_=woven)
+
+        def quantize_weight(woven, name, tag):
+            codes = sbuf([P, H], U32, name + "_codes", tag)
+            scales = sbuf([P, H], U8, name + "_scales")
+            quantize(codes[:], scales[:], woven[:])
+            return codes, scales
+
+        idx = lists.tile([P, S // 16], U16, name="idx")
+        idx2 = lists.tile([P, S // 16], U16, name="idx2")
+        idx3 = lists.tile([P, S // 16], U16, name="idx3")
+        tab_plane = sbuf([P, T], U8, "tab_plane")
+        nc.vector.memset(tab_plane[:].bitcast(I32), 0)
+        load_scale_rows(nc.scalar, tab_plane, tab_scales[0])
+        nc.sync.dma_start(out=idx[:], in_=offs)
+        nc.sync.dma_start(out=idx2[:], in_=offs2)
+        load_plane(0, pieces=2)
+
+        wsc_raw = sbuf([P, 2 * H], U8, "wsc_raw")
+        wsc_plane = sbuf([P, H], U8, "wsc_plane")
+        wo_plane = sbuf([P, 256], U8, "wo_plane")
+        amp_cols = sbuf([P, PACK], F32, "amp_cols")
+        nc.vector.memset(wsc_plane[:].bitcast(I32), 0)
+        nc.vector.memset(wo_plane[:].bitcast(I32), 0)
+
+        wsh_raw = load_weight(wsh, "wsh_raw", "a0")
+        load_plane(1)
+        wp_raw = [load_weight(wp[0:512, :], "wp0_raw", "stage"), load_weight(wp[512:1024, :], "wp1_raw", "a1")]
+        tab = sbuf([P, T], U32, "tab")
+        nc.sync.dma_start(out=tab[:].bitcast(I32), in_=tab_words[0].rearrange("p t i -> p (t i)").bitcast(I32))
+        nc.sync.dma_start(out=wsc_raw[:].bitcast(I32), in_=wsc_words[0].bitcast(I32))
+        load_scale_rows(nc.sync, wsc_plane, wsc_scales[0])
+        nc.sync.dma_start(out=amp_cols[:], in_=amp.rearrange("(p t) -> p t", t=PACK))
+        for k in range(2, 7):
+            load_plane(k)
+        nc.sync.dma_start(out=planes[7][:], in_=base_rows[1, 3])
+        nc.sync.dma_start(out=fresh_last[0][:], in_=xs_rows[1, 3][:, 0:LAST_SPLIT])
+        nc.sync.dma_start(out=fresh_last[1][:], in_=xs_rows[1, 3][:, LAST_SPLIT:S])
+        nc.sync.dma_start(out=idx3[:], in_=offs3)
+        wo_codes = sbuf([P, 256], U32, "wo_codes")
+        nc.sync.dma_start(out=wo_codes[:].bitcast(I32), in_=wo_words[0].rearrange("p c i -> p (c i)").bitcast(I32))
+        load_scale_rows(nc.sync, wo_plane, wo_scales[0])
+        bo_cols = sbuf([P, 2], F32, "bo_cols")
+        with nc.allow_non_contiguous_dma(reason="one bias value a partition"):
+            nc.sync.dma_start(out=bo_cols[:], in_=bo.rearrange("(h p) -> p h", p=P))
+
+        v_scales = sbuf([P, S], U8, "v_scales")
+        nc.vector.tensor_copy(out=v_scales[:], in_=tab_plane[:].indirect(idx[:]))
+        scatter(0, pieces=2)
+        wsc_sorted = sbuf([P, 3 * H], U8, "wsc_sorted", "fresh0")
+        nc.vector.tensor_copy(out=wsc_sorted[:, 0 : 2 * H].bitcast(U16).rearrange("p (t c i) -> p c t i", t=PACK, i=8),
+                              in_=wsc_raw[:].bitcast(U16).rearrange("p (c i t) -> p c t i", t=PACK, i=8))
+        nc.vector.tensor_copy(out=wsc_sorted[:, 2 * H : 3 * H].rearrange("p (t c i) -> p c t i", t=PACK, i=16),
+                              in_=wsc_plane[:].rearrange("p (c i t) -> p c t i", t=PACK, i=16))
+        wsh_woven = weave_weight(wsh_raw, "wsh_woven")
+        wp0_woven = weave_weight(wp_raw[0], "wp0_woven")
+        stage = sbuf([P, 3, T], BF16, "stage")
+        nc.scalar.copy(out=stage[:, 0, :], in_=planes[0][:])
+        wp1_woven = weave_weight(wp_raw[1], "wp1_woven")
+        scatter(1)
+        wsh_codes, wsh_scales = quantize_weight(wsh_woven, "wsh", "fresh1")
+        nc.scalar.copy(out=stage[:, 1, :], in_=planes[1][:])
+        v_words = sbuf([P, S], U32, "v_words")
+        nc.vector.tensor_copy(out=v_words[:], in_=tab[:].indirect(idx[:]))
+        gain = sbuf([P, PACK, S], F32, "gain")
+        for t in range(PACK):
+            for h in range(2):
+                cols = slice(h * BANK, (h + 1) * BANK)
+                sc = bank(2 * t + h, [P, BANK], "sc%d_%d" % (t, h))
+                nc.tensor.matmul_mx(out=sc[:], lhsT=wsc_sorted[:, 256 * t : 256 * (t + 1)].bitcast(FP4X4),
+                                    lhsT_scale=wsc_sorted[:, 2 * H + P * t : 2 * H + P * (t + 1)],
+                                    rhs=v_words[:, cols].bitcast(FP8X4), rhs_scale=v_scales[:, cols],
+                                    start=True, stop=True)
+                nc.scalar.activation(out=gain[:, t, cols], in_=sc[:], func=ACT.Exp, scale=amp_cols[:, t : t + 1])
+        scatter(2)
+        wp_q = [quantize_weight(wp0_woven, "wp0", "fresh2")]
+        nc.scalar.copy(out=stage[:, 2, :], in_=planes[2][:])
+        woven0 = [sbuf([P, HALF * PACK], BF16, "woven0_%d" % h, "a%d" % (2 + h)) for h in range(2)]
+        for h in range(2):
+            nc.scalar.copy(out=woven0[h][:].rearrange("p (c i t) -> p c t i", i=4, t=PACK)[:, :, 0:3, :],
+                           in_=stage[:, :, h * HALF : (h + 1) * HALF].rearrange("p t (c i) -> p c t i", i=4))
+
+        def weave_plane(engine_copy, woven, k, lo, hi):
+            h = lo // HALF
+            engine_copy(out=woven[h][:].rearrange("p (c t) -> p c t", t=PACK)[:, lo - h * HALF : hi - h * HALF, k % PACK],
+                        in_=planes[k][:, lo:hi])
+
+        scatter(3)
+        wp_q.append(quantize_weight(wp1_woven, "wp1", "fresh3"))
+        for h in range(2):
+            weave_plane(nc.scalar.copy, woven0, 3, h * HALF, (h + 1) * HALF)
+        woven1 = [sbuf([P, HALF * PACK], BF16, "woven1_%d" % h) for h in range(2)]
+        page_scales = [sbuf([P, T], U8, "page_scales%d" % a) for a in range(2)]
+        for k in (4, 5, 6):
+            scatter(k)
+            for h in range(2):
+                if k == 6 and h == 0:
+                    nc.scalar.copy(out=woven1[0][:].rearrange("p (c t) -> p c t", t=PACK)[:, :, 2:4],
+                                   in_=planes[k][:, 0:HALF].unsqueeze(2).to_broadcast([P, HALF, 2]))
+                else:
+                    weave_plane(nc.scalar.copy, woven1, k, h * HALF, (h + 1) * HALF)
+        nc.vector.tensor_copy(out=planes[7][:].indirect(idx2[:, 0 : LAST_SPLIT // 16]), in_=fresh_last[0][:])
+        codes0 = sbuf([P, T], U32, "codes0", "fresh7a")
+        for h in range(2):
+            quantize(codes0[:, h * HALF : (h + 1) * HALF], page_scales[0][:, h * HALF : (h + 1) * HALF], woven0[h][:])
+        codes1 = sbuf([P, T], U32, "codes1")
+
+        def page_pass(acc, t, a, c):
+            cols = slice(c * BANK, (c + 1) * BANK)
+            rhs = (codes0, codes1)[a][:, cols]
+            nc.tensor.matmul_mx(out=acc[:], lhsT=wp_q[a][0][:, P * t : P * (t + 1)].bitcast(FP8X4),
+                                lhsT_scale=wp_q[a][1][:, P * t : P * (t + 1)],
+                                rhs=rhs.bitcast(FP8X4), rhs_scale=page_scales[a][:, cols],
+                                start=(a == 0), stop=(a == 1))
+
+        accs = {}
+        for t in range(2):
+            for c in range(4):
+                accs[t, c] = bank(4 * t + c, [P, BANK], "acc%d_%d" % (t, c))
+                page_pass(accs[t, c], t, 0, c)
+        nc.vector.tensor_copy(out=planes[7][:].indirect(idx2[:, LAST_SPLIT // 16 : S // 16]), in_=fresh_last[1][:])
+
+        for c in range(4):
+            weave_plane(nc.vector.tensor_copy if c < 2 else nc.scalar.copy, woven1, 7, c * BANK, (c + 1) * BANK)
+        for c in range(4):
+            cols = slice(c * BANK, (c + 1) * BANK)
+            quantize(codes1[:, cols], page_scales[1][:, cols],
+                     woven1[c // 2][:, (c % 2) * BANK * PACK : (c % 2 + 1) * BANK * PACK])
+        proj = []
+        for t in range(PACK):
+            proj.append(sbuf([P, T], F32, "proj%d" % t, ("a0", "woven1_1", "a2", "a3")[t]))
+            for c in range(4):
+                if t >= 2:
+                    accs[t, c] = bank(4 * (t - 2) + c, [P, BANK], "acc%d_%d" % (t, c))
+                    page_pass(accs[t, c], t, 0, c)
+                page_pass(accs[t, c], t, 1, c)
+                (nc.vector.tensor_copy if (t, c) == (0, 1) else nc.scalar.copy)(out=proj[t][:, c * BANK : (c + 1) * BANK], in_=accs[t, c][:])
+
+        scaled = [sbuf([P, PACK, BANK], F32, "scaled%d" % h, ("woven1_0", "a1")[h]) for h in range(2)]
+        for t in range(PACK):
+            for h in range(2):
+                nc.vector.tensor_tensor(out=scaled[h][:, t, :], in0=proj[t][:].indirect(idx3[:, 32 * h : 32 * (h + 1)]),
+                                        in1=gain[:, t, h * BANK : (h + 1) * BANK], op=ALU.mult)
+        z = sbuf([P, S * PACK], BF16, "z", "stage")
+        z_codes = sbuf([P, S], U32, "z_codes", "fresh0")
+        z_scales = sbuf([P, S], U8, "z_scales")
+        out_rows = out.rearrange("(h p) j -> p h j", p=P)
+
+        def couple(c):
+            sh = bank((0, 1, 2, 3, 4, 5, 0, 1)[c], [P, PACK, P], "sh%d" % c)
+            cols = slice(c * P, (c + 1) * P)
+            for t in range(PACK):
+                nc.tensor.matmul_mx(out=sh[:, t, :], lhsT=wsh_codes[:, P * t : P * (t + 1)].bitcast(FP8X4),
+                                    lhsT_scale=wsh_scales[:, P * t : P * (t + 1)],
+                                    rhs=v_words[:, cols].bitcast(FP8X4), rhs_scale=v_scales[:, cols],
+                                    start=True, stop=True)
+            nc.vector.tensor_tensor(
+                out=z[:, c * P * PACK : (c + 1) * P * PACK].rearrange("p (c i t) -> p c t i", i=4, t=PACK),
+                in0=scaled[c // 4][:, :, (c % 4) * P : (c % 4 + 1) * P].rearrange("p t (c i) -> p c t i", i=4),
+                in1=sh[:].rearrange("p t (c i) -> p c t i", i=4), op=ALU.add)
+
+        def finish(lo, hi, banks, tag, last):
+            cols = slice(lo, hi)
+            quantize(z_codes[:, cols], z_scales[:, cols], z[:, lo * PACK : hi * PACK])
+            result = sbuf([P, 2, hi - lo], F32, "result%d" % lo, tag)
+            for h in range(2):
+                y = bank(banks[h], [P, hi - lo], "y%d_%d" % (lo, h))
+                nc.tensor.matmul_mx(out=y[:], lhsT=wo_codes[:, P * h : P * (h + 1)].bitcast(FP8X4),
+                                    lhsT_scale=wo_plane[:, P * h : P * (h + 1)],
+                                    rhs=z_codes[:, cols].bitcast(FP8X4), rhs_scale=z_scales[:, cols],
+                                    start=True, stop=True)
+                if last and h == 1:
+                    nc.vector.tensor_scalar(out=result[:, h, :], in0=y[:], scalar1=bo_cols[:, h : h + 1], scalar2=None, op0=ALU.add)
+                else:
+                    nc.scalar.activation(out=result[:, h, :], in_=y[:], func=ACT.Identity, bias=bo_cols[:, h : h + 1])
+            nc.sync.dma_start(out=out_rows[:, :, cols], in_=result[:])
+
+        for c in range(5):
+            couple(c)
+        finish(0, 512, (6, 7), "wp0_woven", False)
+        couple(5)
+        couple(6)
+        finish(512, 768, (2, 3), "wp1_woven", False)
+        couple(7)
+        finish(768, 1024, (4, 5), "wsh_woven", True)

@@ -23,7 +23,9 @@ H = 512
 BANK = 512
 HALF = 1024
 AL = 64
-LAST_SPLIT = 768
+ORDER = [(1, 2), (0, 0), (0, 1), (0, 2), (0, 3), (1, 0), (1, 1), (1, 3)]
+CHUNKS = [(1536, 2048), (0, 512), (512, 1024), (1024, 1280), (1280, 1536)]
+BANK_ORDER = [3, 0, 1, 2]
 
 
 def tile_list_tidal_pitch_features_kernel(tc, tab_words, tab_scales, offs, offs2, offs3, xs, base, wp,
@@ -44,23 +46,23 @@ def tile_list_tidal_pitch_features_kernel(tc, tab_words, tab_scales, offs, offs2
             for q in range(4):
                 queue.dma_start(out=plane[32 * q : 32 * q + 4, :].bitcast(I32), in_=rows[4 * q : 4 * q + 4, :].bitcast(I32))
 
+        pins = ctx.enter_context(tc.tile_pool(name="pins", bufs=1))
         base_rows = base.rearrange("(a p j) t -> a j p t", p=P, j=PACK)
         xs_rows = xs.rearrange("(a p j) t -> a j p t", p=P, j=PACK)
-        planes = [sbuf([P, T], F32, "plane%d" % k) for k in range(8)]
-        fresh = [sbuf([P, S], F32, "fresh%d" % k) for k in range(7)]
-        fresh_last = [sbuf([P, LAST_SPLIT], F32, "fresh7a"), sbuf([P, S - LAST_SPLIT], F32, "fresh7b")]
+        planes = {aj: sbuf([P, T], F32, "plane%d%d" % aj) for aj in ORDER}
+        fresh = {aj: sbuf([P, S], F32, "fresh%d%d" % aj) for aj in ORDER}
 
-        def load_plane(k, pieces=1):
-            nc.sync.dma_start(out=planes[k][:], in_=base_rows[k // PACK, k % PACK])
+        def load_plane(aj, pieces=1):
+            nc.sync.dma_start(out=planes[aj][:], in_=base_rows[aj[0], aj[1]])
             w = S // pieces
             for i in range(pieces):
-                nc.sync.dma_start(out=fresh[k][:, i * w : (i + 1) * w], in_=xs_rows[k // PACK, k % PACK][:, i * w : (i + 1) * w])
+                nc.sync.dma_start(out=fresh[aj][:, i * w : (i + 1) * w], in_=xs_rows[aj[0], aj[1]][:, i * w : (i + 1) * w])
 
-        def scatter(k, pieces=1):
+        def scatter(aj, pieces=1):
             w = S // pieces
             for i in range(pieces):
-                nc.vector.tensor_copy(out=planes[k][:].indirect(idx2[:, i * w // 16 : (i + 1) * w // 16]),
-                                      in_=fresh[k][:, i * w : (i + 1) * w])
+                nc.vector.tensor_copy(out=planes[aj][:].indirect(idx2[:, i * w // 16 : (i + 1) * w // 16]),
+                                      in_=fresh[aj][:, i * w : (i + 1) * w])
 
         def load_weight(rows, name, tag):
             raw = sbuf([P, PACK, H], F32, name, tag)
@@ -76,12 +78,6 @@ def tile_list_tidal_pitch_features_kernel(tc, tab_words, tab_scales, offs, offs2
         def quantize(codes, scales, woven):
             nc.vector.quantize_mx(out=codes.bitcast(FP8X4), scales=scales, in_=woven)
 
-        def quantize_weight(woven, name, tag):
-            codes = sbuf([P, H], U32, name + "_codes", tag)
-            scales = sbuf([P, H], U8, name + "_scales")
-            quantize(codes[:], scales[:], woven[:])
-            return codes, scales
-
         idx = lists.tile([P, S // 16], U16, name="idx")
         idx2 = lists.tile([P, S // 16], U16, name="idx2")
         idx3 = lists.tile([P, S // 16], U16, name="idx3")
@@ -90,7 +86,7 @@ def tile_list_tidal_pitch_features_kernel(tc, tab_words, tab_scales, offs, offs2
         load_scale_rows(nc.scalar, tab_plane, tab_scales[0])
         nc.sync.dma_start(out=idx[:], in_=offs)
         nc.sync.dma_start(out=idx2[:], in_=offs2)
-        load_plane(0, pieces=2)
+        load_plane(ORDER[0], pieces=2)
 
         wsc_raw = sbuf([P, 2 * H], U8, "wsc_raw")
         wsc_plane = sbuf([P, H], U8, "wsc_plane")
@@ -99,19 +95,19 @@ def tile_list_tidal_pitch_features_kernel(tc, tab_words, tab_scales, offs, offs2
         nc.vector.memset(wsc_plane[:].bitcast(I32), 0)
         nc.vector.memset(wo_plane[:].bitcast(I32), 0)
 
-        wsh_raw = load_weight(wsh, "wsh_raw", "a0")
-        load_plane(1)
-        wp_raw = [load_weight(wp[0:512, :], "wp0_raw", "stage"), load_weight(wp[512:1024, :], "wp1_raw", "a1")]
-        tab = sbuf([P, T], U32, "tab")
-        nc.sync.dma_start(out=tab[:].bitcast(I32), in_=tab_words[0].rearrange("p t i -> p (t i)").bitcast(I32))
+        load_plane(ORDER[1])
         nc.sync.dma_start(out=wsc_raw[:].bitcast(I32), in_=wsc_words[0].bitcast(I32))
         load_scale_rows(nc.sync, wsc_plane, wsc_scales[0])
         nc.sync.dma_start(out=amp_cols[:], in_=amp.rearrange("(p t) -> p t", t=PACK))
-        for k in range(2, 7):
-            load_plane(k)
-        nc.sync.dma_start(out=planes[7][:], in_=base_rows[1, 3])
-        nc.sync.dma_start(out=fresh_last[0][:], in_=xs_rows[1, 3][:, 0:LAST_SPLIT])
-        nc.sync.dma_start(out=fresh_last[1][:], in_=xs_rows[1, 3][:, LAST_SPLIT:S])
+        tab = sbuf([P, T], U32, "tab")
+        nc.sync.dma_start(out=tab[:].bitcast(I32), in_=tab_words[0].rearrange("p t i -> p (t i)").bitcast(I32))
+        wp_raw = [load_weight(wp[0:512, :], "wp0_raw", "wp0_raw")]
+        load_plane(ORDER[2])
+        wp_raw.append(load_weight(wp[512:1024, :], "wp1_raw", "wp1_raw"))
+        load_plane(ORDER[3])
+        wsh_raw = load_weight(wsh, "wsh_raw", "wsh_raw")
+        for aj in ORDER[4:]:
+            load_plane(aj)
         nc.sync.dma_start(out=idx3[:], in_=offs3)
         wo_codes = sbuf([P, 256], U32, "wo_codes")
         nc.sync.dma_start(out=wo_codes[:].bitcast(I32), in_=wo_words[0].rearrange("p c i -> p (c i)").bitcast(I32))
@@ -120,24 +116,38 @@ def tile_list_tidal_pitch_features_kernel(tc, tab_words, tab_scales, offs, offs2
         with nc.allow_non_contiguous_dma(reason="one bias value a partition"):
             nc.sync.dma_start(out=bo_cols[:], in_=bo.rearrange("(h p) -> p h", p=P))
 
+        woven1 = {}
+        for lo, hi in CHUNKS[:-1]:
+            woven1[lo] = sbuf([P, (hi - lo) * PACK], BF16, "woven1_%d" % lo)
+        lo, hi = CHUNKS[-1]
+        woven1[lo] = pins.tile([P, (hi - lo) * PACK], BF16, name="woven1_last", offset=7168, align_bytes=AL)
+
+        def weave_plane(engine_copy, j, lo, hi):
+            engine_copy(out=woven1[lo][:].rearrange("p (c t) -> p c t", t=PACK)[:, :, j], in_=planes[1, j][:, lo:hi])
+
+        stage = sbuf([P, PACK, T], BF16, "stage")
+
+        def cast(j):
+            nc.scalar.copy(out=stage[:, j, :], in_=planes[0, j][:])
+
         v_scales = sbuf([P, S], U8, "v_scales")
         nc.vector.tensor_copy(out=v_scales[:], in_=tab_plane[:].indirect(idx[:]))
-        scatter(0, pieces=2)
-        wsc_sorted = sbuf([P, 3 * H], U8, "wsc_sorted", "fresh0")
+        scatter((1, 2), pieces=2)
+        lo, hi = CHUNKS[0]
+        nc.scalar.copy(out=woven1[lo][:].rearrange("p (c t) -> p c t", t=PACK)[:, :, 2:4],
+                       in_=planes[1, 2][:, lo:hi].unsqueeze(2).to_broadcast([P, hi - lo, 2]))
+        for lo, hi in CHUNKS[1:]:
+            weave_plane(nc.scalar.copy, 2, lo, hi)
+        wsc_sorted = sbuf([P, 3 * H], U8, "wsc_sorted", "fresh12")
         nc.vector.tensor_copy(out=wsc_sorted[:, 0 : 2 * H].bitcast(U16).rearrange("p (t c i) -> p c t i", t=PACK, i=8),
                               in_=wsc_raw[:].bitcast(U16).rearrange("p (c i t) -> p c t i", t=PACK, i=8))
         nc.vector.tensor_copy(out=wsc_sorted[:, 2 * H : 3 * H].rearrange("p (t c i) -> p c t i", t=PACK, i=16),
                               in_=wsc_plane[:].rearrange("p (c i t) -> p c t i", t=PACK, i=16))
-        wsh_woven = weave_weight(wsh_raw, "wsh_woven")
-        wp0_woven = weave_weight(wp_raw[0], "wp0_woven")
-        stage = sbuf([P, 3, T], BF16, "stage")
-        nc.scalar.copy(out=stage[:, 0, :], in_=planes[0][:])
-        wp1_woven = weave_weight(wp_raw[1], "wp1_woven")
-        scatter(1)
-        wsh_codes, wsh_scales = quantize_weight(wsh_woven, "wsh", "fresh1")
-        nc.scalar.copy(out=stage[:, 1, :], in_=planes[1][:])
+        scatter((0, 0))
+        cast(0)
         v_words = sbuf([P, S], U32, "v_words")
         nc.vector.tensor_copy(out=v_words[:], in_=tab[:].indirect(idx[:]))
+        wp_woven = [weave_weight(wp_raw[0], "wp0_woven")]
         gain = sbuf([P, PACK, S], F32, "gain")
         for t in range(PACK):
             for h in range(2):
@@ -148,77 +158,78 @@ def tile_list_tidal_pitch_features_kernel(tc, tab_words, tab_scales, offs, offs2
                                     rhs=v_words[:, cols].bitcast(FP8X4), rhs_scale=v_scales[:, cols],
                                     start=True, stop=True)
                 nc.scalar.activation(out=gain[:, t, cols], in_=sc[:], func=ACT.Exp, scale=amp_cols[:, t : t + 1])
-        scatter(2)
-        wp_q = [quantize_weight(wp0_woven, "wp0", "fresh2")]
-        nc.scalar.copy(out=stage[:, 2, :], in_=planes[2][:])
-        woven0 = [sbuf([P, HALF * PACK], BF16, "woven0_%d" % h, "a%d" % (2 + h)) for h in range(2)]
-        for h in range(2):
-            nc.scalar.copy(out=woven0[h][:].rearrange("p (c i t) -> p c t i", i=4, t=PACK)[:, :, 0:3, :],
-                           in_=stage[:, :, h * HALF : (h + 1) * HALF].rearrange("p t (c i) -> p c t i", i=4))
+        scatter((0, 1))
+        cast(1)
+        wp_woven.append(weave_weight(wp_raw[1], "wp1_woven"))
+        scatter((0, 2))
+        cast(2)
+        wsh_woven = weave_weight(wsh_raw, "wsh_woven")
+        scatter((0, 3))
+        cast(3)
+        woven0 = [sbuf([P, HALF * PACK], BF16, "woven0_%d" % h, "wp%d_raw" % h) for h in range(2)]
+        for c in range(4):
+            dst = woven0[c // 2][:, (c % 2) * BANK * PACK : (c % 2 + 1) * BANK * PACK].rearrange("p (c t) -> p c t", t=PACK)
+            src = stage[:, :, c * BANK : (c + 1) * BANK].rearrange("p t c -> p c t")
+            if c == 3:
+                nc.scalar.copy(out=dst, in_=src)
+            else:
+                nc.gpsimd.tensor_scalar(out=dst, in0=src, scalar1=1.0, scalar2=0.0, op0=ALU.mult, op1=ALU.add)
+        for j in range(2):
+            scatter((1, j))
+            for lo, hi in CHUNKS:
+                weave_plane(nc.scalar.copy, j, lo, hi)
+        wp_codes = sbuf([P, 2, H], U32, "wp_codes", "fresh11")
+        wp_scales = sbuf([P, 2, H], U8, "wp_scales")
+        for a in range(2):
+            quantize(wp_codes[:, a, :], wp_scales[:, a, :], wp_woven[a][:])
+        scatter((1, 3))
 
-        def weave_plane(engine_copy, woven, k, lo, hi):
-            h = lo // HALF
-            engine_copy(out=woven[h][:].rearrange("p (c t) -> p c t", t=PACK)[:, lo - h * HALF : hi - h * HALF, k % PACK],
-                        in_=planes[k][:, lo:hi])
-
-        scatter(3)
-        wp_q.append(quantize_weight(wp1_woven, "wp1", "fresh3"))
-        for h in range(2):
-            weave_plane(nc.scalar.copy, woven0, 3, h * HALF, (h + 1) * HALF)
-        woven1 = [sbuf([P, HALF * PACK], BF16, "woven1_%d" % h) for h in range(2)]
         page_scales = [sbuf([P, T], U8, "page_scales%d" % a) for a in range(2)]
-        for k in (4, 5, 6):
-            scatter(k)
-            for h in range(2):
-                if k == 6 and h == 0:
-                    nc.scalar.copy(out=woven1[0][:].rearrange("p (c t) -> p c t", t=PACK)[:, :, 2:4],
-                                   in_=planes[k][:, 0:HALF].unsqueeze(2).to_broadcast([P, HALF, 2]))
-                else:
-                    weave_plane(nc.scalar.copy, woven1, k, h * HALF, (h + 1) * HALF)
-        nc.vector.tensor_copy(out=planes[7][:].indirect(idx2[:, 0 : LAST_SPLIT // 16]), in_=fresh_last[0][:])
-        codes0 = sbuf([P, T], U32, "codes0", "fresh7a")
+        codes = [sbuf([P, T], U32, "codes0", "fresh13"), sbuf([P, T], U32, "codes1", "wsh_raw")]
+        for i, (lo, hi) in enumerate(CHUNKS):
+            weave_plane(nc.vector.tensor_copy if i == 0 else nc.scalar.copy, 3, lo, hi)
         for h in range(2):
-            quantize(codes0[:, h * HALF : (h + 1) * HALF], page_scales[0][:, h * HALF : (h + 1) * HALF], woven0[h][:])
-        codes1 = sbuf([P, T], U32, "codes1")
+            quantize(codes[0][:, h * HALF : (h + 1) * HALF], page_scales[0][:, h * HALF : (h + 1) * HALF], woven0[h][:])
 
-        def page_pass(acc, t, a, c):
-            cols = slice(c * BANK, (c + 1) * BANK)
-            rhs = (codes0, codes1)[a][:, cols]
-            nc.tensor.matmul_mx(out=acc[:], lhsT=wp_q[a][0][:, P * t : P * (t + 1)].bitcast(FP8X4),
-                                lhsT_scale=wp_q[a][1][:, P * t : P * (t + 1)],
-                                rhs=rhs.bitcast(FP8X4), rhs_scale=page_scales[a][:, cols],
-                                start=(a == 0), stop=(a == 1))
+        def page_pass(acc, t, a, lo, hi, stop):
+            off = lo % BANK
+            nc.tensor.matmul_mx(out=acc[:, off : off + hi - lo], lhsT=wp_codes[:, a, P * t : P * (t + 1)].bitcast(FP8X4),
+                                lhsT_scale=wp_scales[:, a, P * t : P * (t + 1)],
+                                rhs=codes[a][:, lo:hi].bitcast(FP8X4), rhs_scale=page_scales[a][:, lo:hi],
+                                start=(a == 0), stop=stop)
 
         accs = {}
         for t in range(2):
-            for c in range(4):
+            for c in BANK_ORDER:
                 accs[t, c] = bank(4 * t + c, [P, BANK], "acc%d_%d" % (t, c))
-                page_pass(accs[t, c], t, 0, c)
-        nc.vector.tensor_copy(out=planes[7][:].indirect(idx2[:, LAST_SPLIT // 16 : S // 16]), in_=fresh_last[1][:])
-
-        for c in range(4):
-            weave_plane(nc.vector.tensor_copy if c < 2 else nc.scalar.copy, woven1, 7, c * BANK, (c + 1) * BANK)
-        for c in range(4):
-            cols = slice(c * BANK, (c + 1) * BANK)
-            quantize(codes1[:, cols], page_scales[1][:, cols],
-                     woven1[c // 2][:, (c % 2) * BANK * PACK : (c % 2 + 1) * BANK * PACK])
+                page_pass(accs[t, c], t, 0, c * BANK, (c + 1) * BANK, False)
+        for lo, hi in CHUNKS:
+            quantize(codes[1][:, lo:hi], page_scales[1][:, lo:hi], woven1[lo][:])
+            for t in range(2):
+                page_pass(accs[t, lo // BANK], t, 1, lo, hi, hi % BANK == 0)
+        wsh_codes = pins.tile([P, H], U32, name="wsh_codes", offset=8192, align_bytes=AL)
+        wsh_scales = sbuf([P, H], U8, "wsh_scales")
+        quantize(wsh_codes[:], wsh_scales[:], wsh_woven[:])
         proj = []
         for t in range(PACK):
-            proj.append(sbuf([P, T], F32, "proj%d" % t, ("a0", "woven1_1", "a2", "a3")[t]))
-            for c in range(4):
+            if t == 1:
+                proj.append(pins.tile([P, T], F32, name="proj1", offset=0, align_bytes=AL))
+            else:
+                proj.append(sbuf([P, T], F32, "proj%d" % t, "plane0%d" % t))
+            for c in BANK_ORDER:
                 if t >= 2:
                     accs[t, c] = bank(4 * (t - 2) + c, [P, BANK], "acc%d_%d" % (t, c))
-                    page_pass(accs[t, c], t, 0, c)
-                page_pass(accs[t, c], t, 1, c)
-                (nc.vector.tensor_copy if (t, c) == (0, 1) else nc.scalar.copy)(out=proj[t][:, c * BANK : (c + 1) * BANK], in_=accs[t, c][:])
+                    page_pass(accs[t, c], t, 0, c * BANK, (c + 1) * BANK, False)
+                    page_pass(accs[t, c], t, 1, c * BANK, (c + 1) * BANK, True)
+                (nc.vector.tensor_copy if (t, c) == (0, 2) else nc.scalar.copy)(out=proj[t][:, c * BANK : (c + 1) * BANK], in_=accs[t, c][:])
 
-        scaled = [sbuf([P, PACK, BANK], F32, "scaled%d" % h, ("woven1_0", "a1")[h]) for h in range(2)]
+        scaled = [sbuf([P, PACK, BANK], F32, "scaled%d" % h, "plane1%d" % h) for h in range(2)]
         for t in range(PACK):
             for h in range(2):
                 nc.vector.tensor_tensor(out=scaled[h][:, t, :], in0=proj[t][:].indirect(idx3[:, 32 * h : 32 * (h + 1)]),
                                         in1=gain[:, t, h * BANK : (h + 1) * BANK], op=ALU.mult)
-        z = sbuf([P, S * PACK], BF16, "z", "stage")
-        z_codes = sbuf([P, S], U32, "z_codes", "fresh0")
+        z = sbuf([P, S * PACK], BF16, "z", "tab")
+        z_codes = sbuf([P, S], U32, "z_codes", "fresh00")
         z_scales = sbuf([P, S], U8, "z_scales")
         out_rows = out.rearrange("(h p) j -> p h j", p=P)
 

@@ -1,6 +1,7 @@
 from contextlib import ExitStack
 
 import concourse.mybir as mybir
+from concourse.masks import make_identity
 
 F32 = mybir.dt.float32
 BF16 = mybir.dt.bfloat16
@@ -24,7 +25,9 @@ BANK = 512
 HALF = 1024
 AL = 64
 ORDER = [(1, 2), (0, 0), (0, 1), (0, 2), (0, 3), (1, 0), (1, 1), (1, 3)]
-CHUNKS = [(1536, 2048), (0, 512), (512, 1024), (1024, 1280), (1280, 1536)]
+CHUNKS = [(1536, 2048), (0, 512), (512, 1024), (1024, 1280), (1280, 1408), (1408, 1536)]
+FIRST_PIECES = ((0, 256), (256, S))
+TURNED = 256
 BANK_ORDER = [3, 0, 1, 2]
 
 
@@ -52,17 +55,14 @@ def tile_list_tidal_pitch_features_kernel(tc, tab_words, tab_scales, offs, offs2
         planes = {aj: sbuf([P, T], F32, "plane%d%d" % aj) for aj in ORDER}
         fresh = {aj: sbuf([P, S], F32, "fresh%d%d" % aj) for aj in ORDER}
 
-        def load_plane(aj, pieces=1):
+        def load_plane(aj, pieces=((0, S),)):
             nc.sync.dma_start(out=planes[aj][:], in_=base_rows[aj[0], aj[1]])
-            w = S // pieces
-            for i in range(pieces):
-                nc.sync.dma_start(out=fresh[aj][:, i * w : (i + 1) * w], in_=xs_rows[aj[0], aj[1]][:, i * w : (i + 1) * w])
+            for lo, hi in pieces:
+                nc.sync.dma_start(out=fresh[aj][:, lo:hi], in_=xs_rows[aj[0], aj[1]][:, lo:hi])
 
-        def scatter(aj, pieces=1):
-            w = S // pieces
-            for i in range(pieces):
-                nc.vector.tensor_copy(out=planes[aj][:].indirect(idx2[:, i * w // 16 : (i + 1) * w // 16]),
-                                      in_=fresh[aj][:, i * w : (i + 1) * w])
+        def scatter(aj, pieces=((0, S),)):
+            for lo, hi in pieces:
+                nc.vector.tensor_copy(out=planes[aj][:].indirect(idx2[:, lo // 16 : hi // 16]), in_=fresh[aj][:, lo:hi])
 
         def load_weight(rows, name, tag):
             raw = sbuf([P, PACK, H], F32, name, tag)
@@ -82,18 +82,19 @@ def tile_list_tidal_pitch_features_kernel(tc, tab_words, tab_scales, offs, offs2
         idx2 = lists.tile([P, S // 16], U16, name="idx2")
         idx3 = lists.tile([P, S // 16], U16, name="idx3")
         tab_plane = sbuf([P, T], U8, "tab_plane")
-        nc.vector.memset(tab_plane[:].bitcast(I32), 0)
-        load_scale_rows(nc.scalar, tab_plane, tab_scales[0])
+        nc.gpsimd.memset(tab_plane[:].bitcast(I32), 0)
+        load_scale_rows(nc.sync, tab_plane, tab_scales[0])
         nc.sync.dma_start(out=idx[:], in_=offs)
         nc.sync.dma_start(out=idx2[:], in_=offs2)
-        load_plane(ORDER[0], pieces=2)
+        nc.sync.dma_start(out=idx3[:], in_=offs3)
+        load_plane(ORDER[0], FIRST_PIECES)
 
         wsc_raw = sbuf([P, 2 * H], U8, "wsc_raw")
         wsc_plane = sbuf([P, H], U8, "wsc_plane")
         wo_plane = sbuf([P, 256], U8, "wo_plane")
         amp_cols = sbuf([P, PACK], F32, "amp_cols")
-        nc.vector.memset(wsc_plane[:].bitcast(I32), 0)
-        nc.vector.memset(wo_plane[:].bitcast(I32), 0)
+        nc.gpsimd.memset(wsc_plane[:].bitcast(I32), 0)
+        nc.gpsimd.memset(wo_plane[:].bitcast(I32), 0)
 
         load_plane(ORDER[1])
         nc.sync.dma_start(out=wsc_raw[:].bitcast(I32), in_=wsc_words[0].bitcast(I32))
@@ -108,7 +109,6 @@ def tile_list_tidal_pitch_features_kernel(tc, tab_words, tab_scales, offs, offs2
         wsh_raw = load_weight(wsh, "wsh_raw", "wsh_raw")
         for aj in ORDER[4:]:
             load_plane(aj)
-        nc.sync.dma_start(out=idx3[:], in_=offs3)
         wo_codes = sbuf([P, 256], U32, "wo_codes")
         nc.sync.dma_start(out=wo_codes[:].bitcast(I32), in_=wo_words[0].rearrange("p c i -> p (c i)").bitcast(I32))
         load_scale_rows(nc.sync, wo_plane, wo_scales[0])
@@ -120,11 +120,13 @@ def tile_list_tidal_pitch_features_kernel(tc, tab_words, tab_scales, offs, offs2
         for lo, hi in CHUNKS[:-1]:
             woven1[lo] = sbuf([P, (hi - lo) * PACK], BF16, "woven1_%d" % lo)
         lo, hi = CHUNKS[-1]
-        woven1[lo] = pins.tile([P, (hi - lo) * PACK], BF16, name="woven1_last", offset=7168, align_bytes=AL)
+        woven1[lo] = pins.tile([P, (hi - lo) * PACK], BF16, name="woven1_last", offset=7680, align_bytes=AL)
 
         def weave_plane(engine_copy, j, lo, hi):
             engine_copy(out=woven1[lo][:].rearrange("p (c t) -> p c t", t=PACK)[:, :, j], in_=planes[1, j][:, lo:hi])
 
+        ident = sbuf([P, P], F32, "ident")
+        make_identity(nc, ident[:])
         stage = sbuf([P, PACK, T], BF16, "stage")
 
         def cast(j):
@@ -132,17 +134,17 @@ def tile_list_tidal_pitch_features_kernel(tc, tab_words, tab_scales, offs, offs2
 
         v_scales = sbuf([P, S], U8, "v_scales")
         nc.vector.tensor_copy(out=v_scales[:], in_=tab_plane[:].indirect(idx[:]))
-        scatter((1, 2), pieces=2)
+        scatter((1, 2), FIRST_PIECES)
         lo, hi = CHUNKS[0]
         nc.scalar.copy(out=woven1[lo][:].rearrange("p (c t) -> p c t", t=PACK)[:, :, 2:4],
                        in_=planes[1, 2][:, lo:hi].unsqueeze(2).to_broadcast([P, hi - lo, 2]))
         for lo, hi in CHUNKS[1:]:
             weave_plane(nc.scalar.copy, 2, lo, hi)
-        wsc_sorted = sbuf([P, 3 * H], U8, "wsc_sorted", "fresh12")
-        nc.vector.tensor_copy(out=wsc_sorted[:, 0 : 2 * H].bitcast(U16).rearrange("p (t c i) -> p c t i", t=PACK, i=8),
-                              in_=wsc_raw[:].bitcast(U16).rearrange("p (c i t) -> p c t i", t=PACK, i=8))
-        nc.vector.tensor_copy(out=wsc_sorted[:, 2 * H : 3 * H].rearrange("p (t c i) -> p c t i", t=PACK, i=16),
-                              in_=wsc_plane[:].rearrange("p (c i t) -> p c t i", t=PACK, i=16))
+        wsc_sorted = sbuf([P, 3 * H], U8, "wsc_sorted")
+        nc.gpsimd.tensor_copy(out=wsc_sorted[:, 0 : 2 * H].rearrange("p (t m b) -> p t m b", t=PACK, b=2),
+                              in_=wsc_raw[:].rearrange("p (m t b) -> p t m b", t=PACK, b=2))
+        nc.gpsimd.tensor_copy(out=wsc_sorted[:, 2 * H : 3 * H].rearrange("p (t m) -> p t m", t=PACK),
+                              in_=wsc_plane[:].rearrange("p (m t) -> p t m", t=PACK))
         scatter((0, 0))
         cast(0)
         v_words = sbuf([P, S], U32, "v_words")
@@ -186,69 +188,111 @@ def tile_list_tidal_pitch_features_kernel(tc, tab_words, tab_scales, offs, offs2
 
         page_scales = [sbuf([P, T], U8, "page_scales%d" % a) for a in range(2)]
         codes = [sbuf([P, T], U32, "codes0", "fresh13"), sbuf([P, T], U32, "codes1", "wsh_raw")]
-        for i, (lo, hi) in enumerate(CHUNKS):
-            weave_plane(nc.vector.tensor_copy if i == 0 else nc.scalar.copy, 3, lo, hi)
-        for h in range(2):
-            quantize(codes[0][:, h * HALF : (h + 1) * HALF], page_scales[0][:, h * HALF : (h + 1) * HALF], woven0[h][:])
+        def quantize_page(a, lo, hi, woven):
+            quantize(codes[a][:, lo:hi], page_scales[a][:, lo:hi], woven)
 
-        def page_pass(acc, t, a, lo, hi, stop):
-            off = lo % BANK
-            nc.tensor.matmul_mx(out=acc[:, off : off + hi - lo], lhsT=wp_codes[:, a, P * t : P * (t + 1)].bitcast(FP8X4),
+        def page_pass(acc, t, a, lo, hi, start, stop):
+            nc.tensor.matmul_mx(out=acc, lhsT=wp_codes[:, a, P * t : P * (t + 1)].bitcast(FP8X4),
                                 lhsT_scale=wp_scales[:, a, P * t : P * (t + 1)],
                                 rhs=codes[a][:, lo:hi].bitcast(FP8X4), rhs_scale=page_scales[a][:, lo:hi],
-                                start=(a == 0), stop=stop)
+                                start=start, stop=stop)
 
-        accs = {}
-        for t in range(2):
-            for c in BANK_ORDER:
-                accs[t, c] = bank(4 * t + c, [P, BANK], "acc%d_%d" % (t, c))
-                page_pass(accs[t, c], t, 0, c * BANK, (c + 1) * BANK, False)
-        for lo, hi in CHUNKS:
-            quantize(codes[1][:, lo:hi], page_scales[1][:, lo:hi], woven1[lo][:])
-            for t in range(2):
-                page_pass(accs[t, lo // BANK], t, 1, lo, hi, hi % BANK == 0)
+        quantize_page(0, HALF, T, woven0[1][:])
+        for i, (lo, hi) in enumerate(CHUNKS):
+            weave_plane(nc.vector.tensor_copy if i == 0 else nc.scalar.copy, 3, lo, hi)
+        quantize_page(0, 0, HALF, woven0[0][:])
+        groups = [CHUNKS[0:1], CHUNKS[1:2], CHUNKS[2:3], CHUNKS[3:5], CHUNKS[5:6]]
+        first_accs = [bank(b, [P, g[-1][1] - g[0][0]], "acc0_%d" % b) for b, g in zip((0, 1, 2, 3, 7), groups)]
+        for i in (0, 3, 4, 1, 2):
+            for lo, hi in groups[i]:
+                base_col = groups[i][0][0]
+                page_pass(first_accs[i][:, lo - base_col : hi - base_col], 0, 0, lo, hi, lo == base_col, False)
+        for acc, g in zip(first_accs, groups):
+            for lo, hi in g:
+                quantize_page(1, lo, hi, woven1[lo][:])
+                page_pass(acc[:, lo - g[0][0] : hi - g[0][0]], 0, 1, lo, hi, False, hi == g[-1][1])
         wsh_codes = pins.tile([P, H], U32, name="wsh_codes", offset=8192, align_bytes=AL)
         wsh_scales = sbuf([P, H], U8, "wsh_scales")
         quantize(wsh_codes[:], wsh_scales[:], wsh_woven[:])
-        proj = []
-        for t in range(PACK):
+        proj = [sbuf([P, T], F32, "proj0", "plane00")]
+        for i, (acc, g) in enumerate(zip(first_accs, groups)):
+            (nc.scalar.copy if i < 3 else nc.vector.tensor_copy)(out=proj[0][:, g[0][0] : g[-1][1]], in_=acc[:])
+        for t in range(1, PACK):
             if t == 1:
                 proj.append(pins.tile([P, T], F32, name="proj1", offset=0, align_bytes=AL))
             else:
                 proj.append(sbuf([P, T], F32, "proj%d" % t, "plane0%d" % t))
-            for c in BANK_ORDER:
-                if t >= 2:
-                    accs[t, c] = bank(4 * (t - 2) + c, [P, BANK], "acc%d_%d" % (t, c))
-                    page_pass(accs[t, c], t, 0, c * BANK, (c + 1) * BANK, False)
-                    page_pass(accs[t, c], t, 1, c * BANK, (c + 1) * BANK, True)
-                (nc.vector.tensor_copy if (t, c) == (0, 2) else nc.scalar.copy)(out=proj[t][:, c * BANK : (c + 1) * BANK], in_=accs[t, c][:])
+            for i, c in enumerate(BANK_ORDER):
+                acc = bank(4 * (t % 2) + i, [P, BANK], "acc%d_%d" % (t, c))
+                for a in range(2):
+                    page_pass(acc[:], t, a, c * BANK, (c + 1) * BANK, a == 0, a == 1)
+                nc.scalar.copy(out=proj[t][:, c * BANK : (c + 1) * BANK], in_=acc[:])
 
         scaled = [sbuf([P, PACK, BANK], F32, "scaled%d" % h, "plane1%d" % h) for h in range(2)]
         for t in range(PACK):
             for h in range(2):
                 nc.vector.tensor_tensor(out=scaled[h][:, t, :], in0=proj[t][:].indirect(idx3[:, 32 * h : 32 * (h + 1)]),
                                         in1=gain[:, t, h * BANK : (h + 1) * BANK], op=ALU.mult)
-        z = sbuf([P, S * PACK], BF16, "z", "tab")
         z_codes = sbuf([P, S], U32, "z_codes", "fresh00")
         z_scales = sbuf([P, S], U8, "z_scales")
         out_rows = out.rearrange("(h p) j -> p h j", p=P)
 
-        def couple(c):
-            sh = bank((0, 1, 2, 3, 4, 5, 0, 1)[c], [P, PACK, P], "sh%d" % c)
+        def shift(c, b):
+            sh = bank(b, [P, PACK, P], "sh%d" % c)
             cols = slice(c * P, (c + 1) * P)
             for t in range(PACK):
                 nc.tensor.matmul_mx(out=sh[:, t, :], lhsT=wsh_codes[:, P * t : P * (t + 1)].bitcast(FP8X4),
                                     lhsT_scale=wsh_scales[:, P * t : P * (t + 1)],
                                     rhs=v_words[:, cols].bitcast(FP8X4), rhs_scale=v_scales[:, cols],
                                     start=True, stop=True)
+            return sh
+
+        shifts = {c: shift(c, 2 + c) for c in range(6)}
+        shift_turn = sbuf([P, 2, PACK, P], F32, "shift_turn", "fresh03")
+        turned = [bank(u, [P, 2, 2, P], "turned%d" % u) for u in range(2)]
+
+        def turn(t, src, start, stop):
+            for i in range(2):
+                nc.tensor.matmul(out=turned[t // 2][:, i, t % 2, :], lhsT=src(i), rhs=ident[:],
+                                 is_transpose=True, start=start and i == 0, stop=stop and i == 1)
+
+        def turn_scaled(t, start, stop):
+            turn(t, lambda i: scaled[0][:, t, i * P : (i + 1) * P], start, stop)
+
+        for t in range(3):
+            turn_scaled(t, t % 2 == 0, False)
+        for i in range(2):
+            nc.scalar.copy(out=shift_turn[:, i, :, :], in_=shifts[i][:])
+        for t in range(PACK):
+            turn(t, lambda i: shift_turn[:, i, t, :], False, t == 1)
+        turn_scaled(3, False, True)
+        for c in (6, 7):
+            shifts[c] = shift(c, c - 4)
+        pairs = sbuf([P, 2, 2, 2 * P], BF16, "pairs", "fresh10")
+        for u in range(2):
+            nc.scalar.copy(out=pairs[:, :, u, :].rearrange("j c (p e) -> j c p e", e=2), in_=turned[u][:].rearrange("j c e p -> j c p e"))
+        z_turned = sbuf([P, TURNED * PACK], BF16, "z_turned", "fresh12")
+        for i in range(2):
+            words = bank(i, [P, 2, P], "words%d" % i)
+            for u in range(2):
+                nc.tensor.transpose(words[:, u, :], pairs[:, i, u, :].bitcast(F32), ident[:])
+            nc.scalar.copy(out=z_turned[:].bitcast(F32).rearrange("p (c j u) -> p c j u", c=2, u=2)[:, i, :, :],
+                           in_=words[:].rearrange("p u j -> p j u"))
+
+        z_tiles = [z_turned] + [sbuf([P, TURNED * PACK], BF16, "z%d" % q, tag) for q, tag in ((1, "tab"), (2, "fresh01"), (3, "fresh12"))]
+
+        def z_cols(lo, hi):
+            return z_tiles[lo // TURNED][:, lo % TURNED * PACK : (lo % TURNED + hi - lo) * PACK]
+
+        def couple(c):
             nc.vector.tensor_tensor(
-                out=z[:, c * P * PACK : (c + 1) * P * PACK].rearrange("p (c i t) -> p c t i", i=4, t=PACK),
+                out=z_cols(c * P, (c + 1) * P).rearrange("p (c i t) -> p c t i", i=4, t=PACK),
                 in0=scaled[c // 4][:, :, (c % 4) * P : (c % 4 + 1) * P].rearrange("p t (c i) -> p c t i", i=4),
-                in1=sh[:].rearrange("p t (c i) -> p c t i", i=4), op=ALU.add)
+                in1=shifts[c][:].rearrange("p t (c i) -> p c t i", i=4), op=ALU.add)
 
         def finish(lo, hi, banks, tag, last):
             cols = slice(lo, hi)
-            quantize(z_codes[:, cols], z_scales[:, cols], z[:, lo * PACK : hi * PACK])
+            quantize(z_codes[:, cols], z_scales[:, cols], z_cols(lo, hi))
             result = sbuf([P, 2, hi - lo], F32, "result%d" % lo, tag)
             for h in range(2):
                 y = bank(banks[h], [P, hi - lo], "y%d_%d" % (lo, h))
@@ -262,11 +306,13 @@ def tile_list_tidal_pitch_features_kernel(tc, tab_words, tab_scales, offs, offs2
                     nc.scalar.activation(out=result[:, h, :], in_=y[:], func=ACT.Identity, bias=bo_cols[:, h : h + 1])
             nc.sync.dma_start(out=out_rows[:, :, cols], in_=result[:])
 
-        for c in range(5):
+        for c in (2, 3, 4):
             couple(c)
-        finish(0, 512, (6, 7), "wp0_woven", False)
+        finish(256, 512, (0, 1), "wp0_woven", False)
         couple(5)
+        finish(0, 256, (4, 5), "wp1_woven", False)
         couple(6)
-        finish(512, 768, (2, 3), "wp1_woven", False)
+        finish(512, 768, (0, 1), "wsh_woven", False)
         couple(7)
-        finish(768, 1024, (4, 5), "wsh_woven", True)
+        finish(768, 896, (2, 4), "stage", True)
+        finish(896, 1024, (3, 5), "gain", True)

@@ -27,7 +27,8 @@ AL = 64
 ORDER = [(1, 2), (0, 0), (0, 1), (0, 2), (0, 3), (1, 0), (1, 1), (1, 3)]
 CHUNKS = [(1536, 2048), (0, 512), (512, 1024), (1024, 1280), (1280, 1408), (1408, 1536)]
 FIRST_PIECES = ((0, 256), (256, S))
-TURNED = 256
+TURNED = 3
+PIECE = 256
 BANK_ORDER = [3, 0, 1, 2]
 
 
@@ -73,6 +74,15 @@ def tile_list_tidal_pitch_features_kernel(tc, tab_words, tab_scales, offs, offs2
             woven = sbuf([P, H * PACK], BF16, name)
             nc.scalar.copy(out=woven[:].rearrange("p (t m j) -> p m j t", t=PACK, j=PACK),
                            in_=raw[:].rearrange("p j (m t) -> p m j t", t=PACK))
+            return woven
+
+        def gpsimd_copy(out, in_):
+            nc.gpsimd.tensor_scalar(out=out, in0=in_, scalar1=1.0, scalar2=0.0, op0=ALU.mult, op1=ALU.add)
+
+        def weave_weight_gpsimd(raw, name):
+            woven = sbuf([P, H * PACK], BF16, name)
+            gpsimd_copy(out=woven[:].rearrange("p (t m j) -> p t m j", t=PACK, j=PACK),
+                        in_=raw[:].rearrange("p j (m t) -> p t m j", t=PACK))
             return woven
 
         def quantize(codes, scales, woven):
@@ -162,10 +172,10 @@ def tile_list_tidal_pitch_features_kernel(tc, tab_words, tab_scales, offs, offs2
                 nc.scalar.activation(out=gain[:, t, cols], in_=sc[:], func=ACT.Exp, scale=amp_cols[:, t : t + 1])
         scatter((0, 1))
         cast(1)
-        wp_woven.append(weave_weight(wp_raw[1], "wp1_woven"))
+        wp_woven.append(weave_weight_gpsimd(wp_raw[1], "wp1_woven"))
         scatter((0, 2))
         cast(2)
-        wsh_woven = weave_weight(wsh_raw, "wsh_woven")
+        wsh_woven = weave_weight_gpsimd(wsh_raw, "wsh_woven")
         scatter((0, 3))
         cast(3)
         woven0 = [sbuf([P, HALF * PACK], BF16, "woven0_%d" % h, "wp%d_raw" % h) for h in range(2)]
@@ -175,24 +185,27 @@ def tile_list_tidal_pitch_features_kernel(tc, tab_words, tab_scales, offs, offs2
             if c == 3:
                 nc.scalar.copy(out=dst, in_=src)
             else:
-                nc.gpsimd.tensor_scalar(out=dst, in0=src, scalar1=1.0, scalar2=0.0, op0=ALU.mult, op1=ALU.add)
+                gpsimd_copy(out=dst, in_=src)
         for j in range(2):
             scatter((1, j))
             for lo, hi in CHUNKS:
                 weave_plane(nc.scalar.copy, j, lo, hi)
-        wp_codes = sbuf([P, 2, H], U32, "wp_codes", "fresh11")
         wp_scales = sbuf([P, 2, H], U8, "wp_scales")
-        for a in range(2):
-            quantize(wp_codes[:, a, :], wp_scales[:, a, :], wp_woven[a][:])
+        early_codes = sbuf([P, H + P], U32, "early_codes", "fresh11")
+        quantize(early_codes[:, 0:H], wp_scales[:, 0, :], wp_woven[0][:])
+        quantize(early_codes[:, H : H + P], wp_scales[:, 1, 0:P], wp_woven[1][:, 0 : P * PACK])
         scatter((1, 3))
 
         page_scales = [sbuf([P, T], U8, "page_scales%d" % a) for a in range(2)]
         codes = [sbuf([P, T], U32, "codes0", "fresh13"), sbuf([P, T], U32, "codes1", "wsh_raw")]
+        wp_codes = {(0, t): early_codes[:, P * t : P * (t + 1)] for t in range(PACK)}
+        wp_codes[1, 0] = early_codes[:, H : H + P]
+
         def quantize_page(a, lo, hi, woven):
             quantize(codes[a][:, lo:hi], page_scales[a][:, lo:hi], woven)
 
         def page_pass(acc, t, a, lo, hi, start, stop):
-            nc.tensor.matmul_mx(out=acc, lhsT=wp_codes[:, a, P * t : P * (t + 1)].bitcast(FP8X4),
+            nc.tensor.matmul_mx(out=acc, lhsT=wp_codes[a, t].bitcast(FP8X4),
                                 lhsT_scale=wp_scales[:, a, P * t : P * (t + 1)],
                                 rhs=codes[a][:, lo:hi].bitcast(FP8X4), rhs_scale=page_scales[a][:, lo:hi],
                                 start=start, stop=stop)
@@ -211,12 +224,17 @@ def tile_list_tidal_pitch_features_kernel(tc, tab_words, tab_scales, offs, offs2
             for lo, hi in g:
                 quantize_page(1, lo, hi, woven1[lo][:])
                 page_pass(acc[:, lo - g[0][0] : hi - g[0][0]], 0, 1, lo, hi, False, hi == g[-1][1])
-        wsh_codes = pins.tile([P, H], U32, name="wsh_codes", offset=8192, align_bytes=AL)
+        late_codes = pins.tile([P, 2 * H], U32, name="late_codes", offset=8192, align_bytes=AL)
+        for lo, hi in ((P, 2 * P), (2 * P, H)):
+            quantize(late_codes[:, lo:hi], wp_scales[:, 1, lo:hi], wp_woven[1][:, lo * PACK : hi * PACK])
+        for t in range(1, PACK):
+            wp_codes[1, t] = late_codes[:, P * t : P * (t + 1)]
+        wsh_codes = late_codes[:, H : 2 * H]
         wsh_scales = sbuf([P, H], U8, "wsh_scales")
-        quantize(wsh_codes[:], wsh_scales[:], wsh_woven[:])
+        quantize(wsh_codes, wsh_scales[:], wsh_woven[:])
         proj = [sbuf([P, T], F32, "proj0", "plane00")]
         for i, (acc, g) in enumerate(zip(first_accs, groups)):
-            (nc.scalar.copy if i < 3 else nc.vector.tensor_copy)(out=proj[0][:, g[0][0] : g[-1][1]], in_=acc[:])
+            (nc.scalar.copy if i < 4 else nc.vector.tensor_copy)(out=proj[0][:, g[0][0] : g[-1][1]], in_=acc[:])
         for t in range(1, PACK):
             if t == 1:
                 proj.append(pins.tile([P, T], F32, name="proj1", offset=0, align_bytes=AL))
@@ -247,48 +265,47 @@ def tile_list_tidal_pitch_features_kernel(tc, tab_words, tab_scales, offs, offs2
                                     start=True, stop=True)
             return sh
 
-        shifts = {c: shift(c, 2 + c) for c in range(6)}
-        shift_turn = sbuf([P, 2, PACK, P], F32, "shift_turn", "fresh03")
-        turned = [bank(u, [P, 2, 2, P], "turned%d" % u) for u in range(2)]
+        shifts = {c: shift(c, 3 + c) for c in range(5)}
+        shift_turn = sbuf([P, TURNED, PACK, P], F32, "shift_turn", "plane12")
+        pair_banks = [bank(u, [P, 2, 2, P], "turned%d" % u) for u in range(2)]
+        third_bank = bank(2, [P, PACK, P], "turned2")
 
-        def turn(t, src, start, stop):
-            for i in range(2):
-                nc.tensor.matmul(out=turned[t // 2][:, i, t % 2, :], lhsT=src(i), rhs=ident[:],
-                                 is_transpose=True, start=start and i == 0, stop=stop and i == 1)
-
-        def turn_scaled(t, start, stop):
-            turn(t, lambda i: scaled[0][:, t, i * P : (i + 1) * P], start, stop)
+        def turn(c, t, src, start, stop):
+            acc = pair_banks[t // 2][:, c, t % 2, :] if c < 2 else third_bank[:, t, :]
+            nc.tensor.matmul(out=acc, lhsT=src, rhs=ident[:], is_transpose=True, start=start, stop=stop)
 
         for t in range(3):
-            turn_scaled(t, t % 2 == 0, False)
-        for i in range(2):
-            nc.scalar.copy(out=shift_turn[:, i, :, :], in_=shifts[i][:])
-        for t in range(PACK):
-            turn(t, lambda i: shift_turn[:, i, t, :], False, t == 1)
-        turn_scaled(3, False, True)
-        for c in (6, 7):
-            shifts[c] = shift(c, c - 4)
-        pairs = sbuf([P, 2, 2, 2 * P], BF16, "pairs", "fresh10")
+            for c in range(TURNED):
+                turn(c, t, scaled[0][:, t, c * P : (c + 1) * P], (c, t) in ((0, 0), (0, 2), (2, 0)), False)
+        for c in range(TURNED):
+            nc.scalar.copy(out=shift_turn[:, c, :, :], in_=shifts[c][:])
+        for c, t in [(c, t) for t in range(PACK) for c in range(2)] + [(2, t) for t in range(PACK)]:
+            turn(c, t, shift_turn[:, c, t, :], False, (c, t) == (1, 1))
+        for c in range(TURNED):
+            turn(c, 3, scaled[0][:, 3, c * P : (c + 1) * P], False, c > 0)
+        for c in (5, 6, 7):
+            shifts[c] = shift(c, c - 2)
+        pairs = sbuf([P, TURNED, 2, 2 * P], BF16, "pairs", "fresh10")
         for u in range(2):
-            nc.scalar.copy(out=pairs[:, :, u, :].rearrange("j c (p e) -> j c p e", e=2), in_=turned[u][:].rearrange("j c e p -> j c p e"))
-        z_turned = sbuf([P, TURNED * PACK], BF16, "z_turned", "fresh12")
-        for i in range(2):
-            words = bank(i, [P, 2, P], "words%d" % i)
+            nc.scalar.copy(out=pairs[:, 0:2, u, :].rearrange("j c (p e) -> j c p e", e=2), in_=pair_banks[u][:].rearrange("j c e p -> j c p e"))
+        nc.scalar.copy(out=pairs[:, 2, :, :].rearrange("j u (p e) -> j u p e", e=2), in_=third_bank[:].rearrange("j (u e) p -> j u p e", e=2))
+        z_tiles = [sbuf([P, PIECE * PACK], BF16, "z%d" % q, tag) for q, tag in enumerate(("fresh12", "tab", "fresh01"))]
+        for c in range(TURNED):
+            words = bank(c, [P, 2, P], "words%d" % c)
             for u in range(2):
-                nc.tensor.transpose(words[:, u, :], pairs[:, i, u, :].bitcast(F32), ident[:])
-            nc.scalar.copy(out=z_turned[:].bitcast(F32).rearrange("p (c j u) -> p c j u", c=2, u=2)[:, i, :, :],
+                nc.tensor.transpose(words[:, u, :], pairs[:, c, u, :].bitcast(F32), ident[:])
+            nc.scalar.copy(out=z_tiles[c // 2][:].bitcast(F32).rearrange("p (c j u) -> p c j u", c=2, u=2)[:, c % 2, :, :],
                            in_=words[:].rearrange("p u j -> p j u"))
-
-        z_tiles = [z_turned] + [sbuf([P, TURNED * PACK], BF16, "z%d" % q, tag) for q, tag in ((1, "tab"), (2, "fresh01"), (3, "fresh12"))]
+        z_tiles.append(sbuf([P, PIECE * PACK], BF16, "z3", "fresh12"))
 
         def z_cols(lo, hi):
-            return z_tiles[lo // TURNED][:, lo % TURNED * PACK : (lo % TURNED + hi - lo) * PACK]
+            return z_tiles[lo // PIECE][:, lo % PIECE * PACK : (lo % PIECE + hi - lo) * PACK]
 
         def couple(c):
             nc.vector.tensor_tensor(
-                out=z_cols(c * P, (c + 1) * P).rearrange("p (c i t) -> p c t i", i=4, t=PACK),
-                in0=scaled[c // 4][:, :, (c % 4) * P : (c % 4 + 1) * P].rearrange("p t (c i) -> p c t i", i=4),
-                in1=shifts[c][:].rearrange("p t (c i) -> p c t i", i=4), op=ALU.add)
+                out=z_cols(c * P, (c + 1) * P).rearrange("p (c i t) -> p c t i", i=2, t=PACK),
+                in0=scaled[c // 4][:, :, (c % 4) * P : (c % 4 + 1) * P].rearrange("p t (c i) -> p c t i", i=2),
+                in1=shifts[c][:].rearrange("p t (c i) -> p c t i", i=2), op=ALU.add)
 
         def finish(lo, hi, banks, tag, last):
             cols = slice(lo, hi)
@@ -304,15 +321,18 @@ def tile_list_tidal_pitch_features_kernel(tc, tab_words, tab_scales, offs, offs2
                     nc.vector.tensor_scalar(out=result[:, h, :], in0=y[:], scalar1=bo_cols[:, h : h + 1], scalar2=None, op0=ALU.add)
                 else:
                     nc.scalar.activation(out=result[:, h, :], in_=y[:], func=ACT.Identity, bias=bo_cols[:, h : h + 1])
-            nc.sync.dma_start(out=out_rows[:, :, cols], in_=result[:])
+            if hi == S:
+                nc.scalar.dma_start(out=out_rows[:, 0, cols], in_=result[:, 0, :])
+                nc.sync.dma_start(out=out_rows[:, 1, cols], in_=result[:, 1, :])
+            else:
+                nc.sync.dma_start(out=out_rows[:, :, cols], in_=result[:])
 
-        for c in (2, 3, 4):
+        for c in (3, 4, 5):
             couple(c)
-        finish(256, 512, (0, 1), "wp0_woven", False)
-        couple(5)
-        finish(0, 256, (4, 5), "wp1_woven", False)
+        finish(0, 256, (0, 6), "wp0_woven", False)
+        finish(512, 768, (1, 2), "wp1_woven", False)
         couple(6)
-        finish(512, 768, (0, 1), "wsh_woven", False)
+        finish(256, 512, (7, 3), "wsh_woven", False)
         couple(7)
-        finish(768, 896, (2, 4), "stage", True)
-        finish(896, 1024, (3, 5), "gain", True)
+        finish(768, 896, (4, 1), "stage", True)
+        finish(896, 1024, (5, 2), "gain", True)

@@ -21,15 +21,20 @@ PACK = 4
 T = 2048
 S = 1024
 H = 512
+N = 256
+GROUP = 16
+SCALE_ROWS = 16
 BANK = 512
-HALF = 1024
+HALF = T // 2
 AL = 64
+
 ORDER = [(1, 2), (0, 0), (0, 1), (0, 2), (0, 3), (1, 0), (1, 1), (1, 3)]
+FIRST_PIECES = ((0, S // 4), (S // 4, S))
 CHUNKS = [(1536, 2048), (0, 512), (512, 1024), (1024, 1280), (1280, 1408), (1408, 1536)]
-FIRST_PIECES = ((0, 256), (256, S))
-TURNED = 3
-PIECE = 256
 BANK_ORDER = [3, 0, 1, 2]
+GPSIMD_RANGES = 3
+TURNED = 3
+PIECE = 2 * P
 
 
 def tile_list_tidal_pitch_features_kernel(tc, tab_words, tab_scales, offs, offs2, offs3, xs, base, wp,
@@ -39,6 +44,7 @@ def tile_list_tidal_pitch_features_kernel(tc, tab_words, tab_scales, offs, offs2
         lists = ctx.enter_context(tc.tile_pool(name="lists", bufs=1))
         sb = ctx.enter_context(tc.tile_pool(name="sb", bufs=1))
         psum = ctx.enter_context(tc.psum_pool(name="psum", bufs=1))
+        placed = ctx.enter_context(tc.tile_pool(name="placed", bufs=1))
 
         def sbuf(shape, dtype, name, tag=None):
             return sb.tile(shape, dtype, name=name, tag=tag or name, align_bytes=AL)
@@ -46,11 +52,10 @@ def tile_list_tidal_pitch_features_kernel(tc, tab_words, tab_scales, offs, offs2
         def bank(b, shape, name):
             return psum.tile(shape, F32, name=name, tag="bank%d" % b)
 
-        def load_scale_rows(queue, plane, rows):
+        def move_scale_rows(queue, scales, rows):
             for q in range(4):
-                queue.dma_start(out=plane[32 * q : 32 * q + 4, :].bitcast(I32), in_=rows[4 * q : 4 * q + 4, :].bitcast(I32))
+                queue.dma_start(out=scales[32 * q : 32 * q + 4, :].bitcast(I32), in_=rows[4 * q : 4 * q + 4, :].bitcast(I32))
 
-        pins = ctx.enter_context(tc.tile_pool(name="pins", bufs=1))
         base_rows = base.rearrange("(a p j) t -> a j p t", p=P, j=PACK)
         xs_rows = xs.rearrange("(a p j) t -> a j p t", p=P, j=PACK)
         planes = {aj: sbuf([P, T], F32, "plane%d%d" % aj) for aj in ORDER}
@@ -63,74 +68,69 @@ def tile_list_tidal_pitch_features_kernel(tc, tab_words, tab_scales, offs, offs2
 
         def scatter(aj, pieces=((0, S),)):
             for lo, hi in pieces:
-                nc.vector.tensor_copy(out=planes[aj][:].indirect(idx2[:, lo // 16 : hi // 16]), in_=fresh[aj][:, lo:hi])
+                nc.vector.tensor_copy(out=planes[aj][:].indirect(idx2[:, lo // GROUP : hi // GROUP]), in_=fresh[aj][:, lo:hi])
 
-        def load_weight(rows, name, tag):
-            raw = sbuf([P, PACK, H], F32, name, tag)
+        def load_weight(rows, name):
+            raw = sbuf([P, PACK, H], F32, name)
             nc.sync.dma_start(out=raw[:], in_=rows.rearrange("(p j) r -> p j r", j=PACK))
             return raw
-
-        def weave_weight(raw, name):
-            woven = sbuf([P, H * PACK], BF16, name)
-            nc.scalar.copy(out=woven[:].rearrange("p (t m j) -> p m j t", t=PACK, j=PACK),
-                           in_=raw[:].rearrange("p j (m t) -> p m j t", t=PACK))
-            return woven
 
         def gpsimd_copy(out, in_):
             nc.gpsimd.tensor_scalar(out=out, in0=in_, scalar1=1.0, scalar2=0.0, op0=ALU.mult, op1=ALU.add)
 
-        def weave_weight_gpsimd(raw, name):
+        def weave_weight(engine_copy, raw, name, walk):
             woven = sbuf([P, H * PACK], BF16, name)
-            gpsimd_copy(out=woven[:].rearrange("p (t m j) -> p t m j", t=PACK, j=PACK),
-                        in_=raw[:].rearrange("p j (m t) -> p t m j", t=PACK))
+            engine_copy(out=woven[:].rearrange("p (t m j) -> " + walk, t=PACK, j=PACK),
+                        in_=raw[:].rearrange("p j (m t) -> " + walk, t=PACK))
             return woven
 
         def quantize(codes, scales, woven):
             nc.vector.quantize_mx(out=codes.bitcast(FP8X4), scales=scales, in_=woven)
 
-        idx = lists.tile([P, S // 16], U16, name="idx")
-        idx2 = lists.tile([P, S // 16], U16, name="idx2")
-        idx3 = lists.tile([P, S // 16], U16, name="idx3")
-        tab_plane = sbuf([P, T], U8, "tab_plane")
-        nc.gpsimd.memset(tab_plane[:].bitcast(I32), 0)
-        load_scale_rows(nc.sync, tab_plane, tab_scales[0])
+        idx = lists.tile([P, S // GROUP], U16, name="idx")
+        idx2 = lists.tile([P, S // GROUP], U16, name="idx2")
+        idx3 = lists.tile([P, S // GROUP], U16, name="idx3")
+        tab_rows = sbuf([P, T], U8, "tab_rows")
+        nc.gpsimd.memset(tab_rows[0 : P - SCALE_ROWS, :].bitcast(I32), 0)
+        nc.sync.dma_start(out=tab_rows[P - SCALE_ROWS : P, :].bitcast(I32), in_=tab_scales[0].bitcast(I32))
         nc.sync.dma_start(out=idx[:], in_=offs)
         nc.sync.dma_start(out=idx2[:], in_=offs2)
-        nc.sync.dma_start(out=idx3[:], in_=offs3)
         load_plane(ORDER[0], FIRST_PIECES)
 
         wsc_raw = sbuf([P, 2 * H], U8, "wsc_raw")
-        wsc_plane = sbuf([P, H], U8, "wsc_plane")
-        wo_plane = sbuf([P, 256], U8, "wo_plane")
+        wsc_raw_scales = sbuf([P, H], U8, "wsc_raw_scales")
+        wo_block_scales = sbuf([P, N], U8, "wo_block_scales")
         amp_cols = sbuf([P, PACK], F32, "amp_cols")
-        nc.gpsimd.memset(wsc_plane[:].bitcast(I32), 0)
-        nc.gpsimd.memset(wo_plane[:].bitcast(I32), 0)
+        nc.gpsimd.memset(wsc_raw_scales[:].bitcast(I32), 0)
+        nc.gpsimd.memset(wo_block_scales[:].bitcast(I32), 0)
 
         load_plane(ORDER[1])
         nc.sync.dma_start(out=wsc_raw[:].bitcast(I32), in_=wsc_words[0].bitcast(I32))
-        load_scale_rows(nc.sync, wsc_plane, wsc_scales[0])
+        move_scale_rows(nc.sync, wsc_raw_scales, wsc_scales[0])
         nc.sync.dma_start(out=amp_cols[:], in_=amp.rearrange("(p t) -> p t", t=PACK))
         tab = sbuf([P, T], U32, "tab")
         nc.sync.dma_start(out=tab[:].bitcast(I32), in_=tab_words[0].rearrange("p t i -> p (t i)").bitcast(I32))
-        wp_raw = [load_weight(wp[0:512, :], "wp0_raw", "wp0_raw")]
+        wp_raw = [load_weight(wp[0:H, :], "wp0_raw")]
         load_plane(ORDER[2])
-        wp_raw.append(load_weight(wp[512:1024, :], "wp1_raw", "wp1_raw"))
+        wp_raw.append(load_weight(wp[H : 2 * H, :], "wp1_raw"))
         load_plane(ORDER[3])
-        wsh_raw = load_weight(wsh, "wsh_raw", "wsh_raw")
+        wsh_raw = load_weight(wsh, "wsh_raw")
         for aj in ORDER[4:]:
             load_plane(aj)
-        wo_codes = sbuf([P, 256], U32, "wo_codes")
+        nc.sync.dma_start(out=idx3[:], in_=offs3)
+        wo_codes = sbuf([P, N], U32, "wo_codes")
         nc.sync.dma_start(out=wo_codes[:].bitcast(I32), in_=wo_words[0].rearrange("p c i -> p (c i)").bitcast(I32))
-        load_scale_rows(nc.sync, wo_plane, wo_scales[0])
+        move_scale_rows(nc.sync, wo_block_scales, wo_scales[0])
         bo_cols = sbuf([P, 2], F32, "bo_cols")
         with nc.allow_non_contiguous_dma(reason="one bias value a partition"):
             nc.sync.dma_start(out=bo_cols[:], in_=bo.rearrange("(h p) -> p h", p=P))
 
+        border = T * 4
         woven1 = {}
         for lo, hi in CHUNKS[:-1]:
             woven1[lo] = sbuf([P, (hi - lo) * PACK], BF16, "woven1_%d" % lo)
         lo, hi = CHUNKS[-1]
-        woven1[lo] = pins.tile([P, (hi - lo) * PACK], BF16, name="woven1_last", offset=7680, align_bytes=AL)
+        woven1[lo] = placed.tile([P, (hi - lo) * PACK], BF16, name="woven1_last", offset=border - (hi - lo) * PACK, align_bytes=AL)
 
         def weave_plane(engine_copy, j, lo, hi):
             engine_copy(out=woven1[lo][:].rearrange("p (c t) -> p c t", t=PACK)[:, :, j], in_=planes[1, j][:, lo:hi])
@@ -139,11 +139,14 @@ def tile_list_tidal_pitch_features_kernel(tc, tab_words, tab_scales, offs, offs2
         make_identity(nc, ident[:])
         stage = sbuf([P, PACK, T], BF16, "stage")
 
-        def cast(j):
+        def stage_plane(j):
             nc.scalar.copy(out=stage[:, j, :], in_=planes[0, j][:])
 
+        v_rows = sbuf([P, S], U8, "v_rows")
+        nc.vector.tensor_copy(out=v_rows[:], in_=tab_rows[:].indirect(idx[:]))
         v_scales = sbuf([P, S], U8, "v_scales")
-        nc.vector.tensor_copy(out=v_scales[:], in_=tab_plane[:].indirect(idx[:]))
+        nc.gpsimd.memset(v_scales[:].bitcast(I32), 0)
+        move_scale_rows(nc.scalar, v_scales, v_rows[P - SCALE_ROWS : P, :])
         scatter((1, 2), FIRST_PIECES)
         lo, hi = CHUNKS[0]
         nc.scalar.copy(out=woven1[lo][:].rearrange("p (c t) -> p c t", t=PACK)[:, :, 2:4],
@@ -154,38 +157,35 @@ def tile_list_tidal_pitch_features_kernel(tc, tab_words, tab_scales, offs, offs2
         nc.gpsimd.tensor_copy(out=wsc_sorted[:, 0 : 2 * H].rearrange("p (t m b) -> p t m b", t=PACK, b=2),
                               in_=wsc_raw[:].rearrange("p (m t b) -> p t m b", t=PACK, b=2))
         nc.gpsimd.tensor_copy(out=wsc_sorted[:, 2 * H : 3 * H].rearrange("p (t m) -> p t m", t=PACK),
-                              in_=wsc_plane[:].rearrange("p (m t) -> p t m", t=PACK))
+                              in_=wsc_raw_scales[:].rearrange("p (m t) -> p t m", t=PACK))
         scatter((0, 0))
-        cast(0)
+        stage_plane(0)
         v_words = sbuf([P, S], U32, "v_words")
         nc.vector.tensor_copy(out=v_words[:], in_=tab[:].indirect(idx[:]))
-        wp_woven = [weave_weight(wp_raw[0], "wp0_woven")]
+        wp_woven = [weave_weight(nc.scalar.copy, wp_raw[0], "wp0_woven", "p m j t")]
         gain = sbuf([P, PACK, S], F32, "gain")
         for t in range(PACK):
-            for h in range(2):
+            for h in range(S // BANK):
                 cols = slice(h * BANK, (h + 1) * BANK)
                 sc = bank(2 * t + h, [P, BANK], "sc%d_%d" % (t, h))
-                nc.tensor.matmul_mx(out=sc[:], lhsT=wsc_sorted[:, 256 * t : 256 * (t + 1)].bitcast(FP4X4),
+                nc.tensor.matmul_mx(out=sc[:], lhsT=wsc_sorted[:, 2 * P * t : 2 * P * (t + 1)].bitcast(FP4X4),
                                     lhsT_scale=wsc_sorted[:, 2 * H + P * t : 2 * H + P * (t + 1)],
                                     rhs=v_words[:, cols].bitcast(FP8X4), rhs_scale=v_scales[:, cols],
                                     start=True, stop=True)
                 nc.scalar.activation(out=gain[:, t, cols], in_=sc[:], func=ACT.Exp, scale=amp_cols[:, t : t + 1])
         scatter((0, 1))
-        cast(1)
-        wp_woven.append(weave_weight_gpsimd(wp_raw[1], "wp1_woven"))
+        stage_plane(1)
+        wp_woven.append(weave_weight(gpsimd_copy, wp_raw[1], "wp1_woven", "p t m j"))
         scatter((0, 2))
-        cast(2)
-        wsh_woven = weave_weight_gpsimd(wsh_raw, "wsh_woven")
+        stage_plane(2)
+        wsh_woven = weave_weight(gpsimd_copy, wsh_raw, "wsh_woven", "p t m j")
         scatter((0, 3))
-        cast(3)
+        stage_plane(3)
         woven0 = [sbuf([P, HALF * PACK], BF16, "woven0_%d" % h, "wp%d_raw" % h) for h in range(2)]
-        for c in range(4):
-            dst = woven0[c // 2][:, (c % 2) * BANK * PACK : (c % 2 + 1) * BANK * PACK].rearrange("p (c t) -> p c t", t=PACK)
-            src = stage[:, :, c * BANK : (c + 1) * BANK].rearrange("p t c -> p c t")
-            if c == 3:
-                nc.scalar.copy(out=dst, in_=src)
-            else:
-                gpsimd_copy(out=dst, in_=src)
+        for c in range(T // BANK):
+            (gpsimd_copy if c < GPSIMD_RANGES else nc.scalar.copy)(
+                out=woven0[c // 2][:, (c % 2) * BANK * PACK : (c % 2 + 1) * BANK * PACK].rearrange("p (c t) -> p c t", t=PACK),
+                in_=stage[:, :, c * BANK : (c + 1) * BANK].rearrange("p t c -> p c t"))
         for j in range(2):
             scatter((1, j))
             for lo, hi in CHUNKS:
@@ -197,34 +197,34 @@ def tile_list_tidal_pitch_features_kernel(tc, tab_words, tab_scales, offs, offs2
         scatter((1, 3))
 
         page_scales = [sbuf([P, T], U8, "page_scales%d" % a) for a in range(2)]
-        codes = [sbuf([P, T], U32, "codes0", "fresh13"), sbuf([P, T], U32, "codes1", "wsh_raw")]
+        page_codes = [sbuf([P, T], U32, "page_codes0", "fresh13"), sbuf([P, T], U32, "page_codes1", "wsh_raw")]
         wp_codes = {(0, t): early_codes[:, P * t : P * (t + 1)] for t in range(PACK)}
         wp_codes[1, 0] = early_codes[:, H : H + P]
 
         def quantize_page(a, lo, hi, woven):
-            quantize(codes[a][:, lo:hi], page_scales[a][:, lo:hi], woven)
+            quantize(page_codes[a][:, lo:hi], page_scales[a][:, lo:hi], woven)
 
         def page_pass(acc, t, a, lo, hi, start, stop):
             nc.tensor.matmul_mx(out=acc, lhsT=wp_codes[a, t].bitcast(FP8X4),
                                 lhsT_scale=wp_scales[:, a, P * t : P * (t + 1)],
-                                rhs=codes[a][:, lo:hi].bitcast(FP8X4), rhs_scale=page_scales[a][:, lo:hi],
+                                rhs=page_codes[a][:, lo:hi].bitcast(FP8X4), rhs_scale=page_scales[a][:, lo:hi],
                                 start=start, stop=stop)
 
         quantize_page(0, HALF, T, woven0[1][:])
         for i, (lo, hi) in enumerate(CHUNKS):
             weave_plane(nc.vector.tensor_copy if i == 0 else nc.scalar.copy, 3, lo, hi)
         quantize_page(0, 0, HALF, woven0[0][:])
-        groups = [CHUNKS[0:1], CHUNKS[1:2], CHUNKS[2:3], CHUNKS[3:5], CHUNKS[5:6]]
-        first_accs = [bank(b, [P, g[-1][1] - g[0][0]], "acc0_%d" % b) for b, g in zip((0, 1, 2, 3, 7), groups)]
-        for i in (0, 3, 4, 1, 2):
-            for lo, hi in groups[i]:
-                base_col = groups[i][0][0]
-                page_pass(first_accs[i][:, lo - base_col : hi - base_col], 0, 0, lo, hi, lo == base_col, False)
-        for acc, g in zip(first_accs, groups):
-            for lo, hi in g:
+        shares = [CHUNKS[0:1], CHUNKS[1:2], CHUNKS[2:3], CHUNKS[3:5], CHUNKS[5:6]]
+        first_accs = [bank(b, [P, share[-1][1] - share[0][0]], "acc0_%d" % b) for b, share in zip((0, 1, 2, 3, 7), shares)]
+        upper_half_first = sorted(zip(first_accs, shares), key=lambda pair: pair[1][0][0] < HALF)
+        for acc, share in upper_half_first:
+            for lo, hi in share:
+                page_pass(acc[:, lo - share[0][0] : hi - share[0][0]], 0, 0, lo, hi, lo == share[0][0], False)
+        for acc, share in zip(first_accs, shares):
+            for lo, hi in share:
                 quantize_page(1, lo, hi, woven1[lo][:])
-                page_pass(acc[:, lo - g[0][0] : hi - g[0][0]], 0, 1, lo, hi, False, hi == g[-1][1])
-        late_codes = pins.tile([P, 2 * H], U32, name="late_codes", offset=8192, align_bytes=AL)
+                page_pass(acc[:, lo - share[0][0] : hi - share[0][0]], 0, 1, lo, hi, False, hi == share[-1][1])
+        late_codes = placed.tile([P, 2 * H], U32, name="late_codes", offset=border, align_bytes=AL)
         for lo, hi in ((P, 2 * P), (2 * P, H)):
             quantize(late_codes[:, lo:hi], wp_scales[:, 1, lo:hi], wp_woven[1][:, lo * PACK : hi * PACK])
         for t in range(1, PACK):
@@ -233,11 +233,11 @@ def tile_list_tidal_pitch_features_kernel(tc, tab_words, tab_scales, offs, offs2
         wsh_scales = sbuf([P, H], U8, "wsh_scales")
         quantize(wsh_codes, wsh_scales[:], wsh_woven[:])
         proj = [sbuf([P, T], F32, "proj0", "plane00")]
-        for i, (acc, g) in enumerate(zip(first_accs, groups)):
-            (nc.scalar.copy if i < 4 else nc.vector.tensor_copy)(out=proj[0][:, g[0][0] : g[-1][1]], in_=acc[:])
+        for acc, share in zip(first_accs, shares):
+            (nc.vector.tensor_copy if share is shares[-1] else nc.scalar.copy)(out=proj[0][:, share[0][0] : share[-1][1]], in_=acc[:])
         for t in range(1, PACK):
             if t == 1:
-                proj.append(pins.tile([P, T], F32, name="proj1", offset=0, align_bytes=AL))
+                proj.append(placed.tile([P, T], F32, name="proj1", offset=0, align_bytes=AL))
             else:
                 proj.append(sbuf([P, T], F32, "proj%d" % t, "plane0%d" % t))
             for i, c in enumerate(BANK_ORDER):
@@ -246,11 +246,11 @@ def tile_list_tidal_pitch_features_kernel(tc, tab_words, tab_scales, offs, offs2
                     page_pass(acc[:], t, a, c * BANK, (c + 1) * BANK, a == 0, a == 1)
                 nc.scalar.copy(out=proj[t][:, c * BANK : (c + 1) * BANK], in_=acc[:])
 
-        scaled = [sbuf([P, PACK, BANK], F32, "scaled%d" % h, "plane1%d" % h) for h in range(2)]
+        scaled = sbuf([P, PACK, S], F32, "scaled", "stage")
         for t in range(PACK):
-            for h in range(2):
-                nc.vector.tensor_tensor(out=scaled[h][:, t, :], in0=proj[t][:].indirect(idx3[:, 32 * h : 32 * (h + 1)]),
-                                        in1=gain[:, t, h * BANK : (h + 1) * BANK], op=ALU.mult)
+            for lo, hi in ((0, S),) if t < PACK - 1 else ((0, S // 2), (S // 2, S)):
+                nc.vector.tensor_tensor(out=scaled[:, t, lo:hi], in0=proj[t][:].indirect(idx3[:, lo // GROUP : hi // GROUP]),
+                                        in1=gain[:, t, lo:hi], op=ALU.mult)
         z_codes = sbuf([P, S], U32, "z_codes", "fresh00")
         z_scales = sbuf([P, S], U8, "z_scales")
         out_rows = out.rearrange("(h p) j -> p h j", p=P)
@@ -265,8 +265,8 @@ def tile_list_tidal_pitch_features_kernel(tc, tab_words, tab_scales, offs, offs2
                                     start=True, stop=True)
             return sh
 
-        shifts = {c: shift(c, 3 + c) for c in range(5)}
-        shift_turn = sbuf([P, TURNED, PACK, P], F32, "shift_turn", "plane12")
+        shifts = {c: shift(c, TURNED + c) for c in range(8 - TURNED)}
+        shift_sbuf = sbuf([P, TURNED, PACK, P], F32, "shift_sbuf", "plane12")
         pair_banks = [bank(u, [P, 2, 2, P], "turned%d" % u) for u in range(2)]
         third_bank = bank(2, [P, PACK, P], "turned2")
 
@@ -274,21 +274,24 @@ def tile_list_tidal_pitch_features_kernel(tc, tab_words, tab_scales, offs, offs2
             acc = pair_banks[t // 2][:, c, t % 2, :] if c < 2 else third_bank[:, t, :]
             nc.tensor.matmul(out=acc, lhsT=src, rhs=ident[:], is_transpose=True, start=start, stop=stop)
 
-        for t in range(3):
+        opens_a_bank = ((0, 0), (0, 2), (2, 0))
+        for t in range(PACK - 1):
             for c in range(TURNED):
-                turn(c, t, scaled[0][:, t, c * P : (c + 1) * P], (c, t) in ((0, 0), (0, 2), (2, 0)), False)
+                turn(c, t, scaled[:, t, c * P : (c + 1) * P], (c, t) in opens_a_bank, False)
         for c in range(TURNED):
-            nc.scalar.copy(out=shift_turn[:, c, :, :], in_=shifts[c][:])
+            nc.scalar.copy(out=shift_sbuf[:, c, :, :], in_=shifts[c][:])
         for c, t in [(c, t) for t in range(PACK) for c in range(2)] + [(2, t) for t in range(PACK)]:
-            turn(c, t, shift_turn[:, c, t, :], False, (c, t) == (1, 1))
+            turn(c, t, shift_sbuf[:, c, t, :], False, (c, t) == (1, 1))
         for c in range(TURNED):
-            turn(c, 3, scaled[0][:, 3, c * P : (c + 1) * P], False, c > 0)
-        for c in (5, 6, 7):
-            shifts[c] = shift(c, c - 2)
+            turn(c, PACK - 1, scaled[:, PACK - 1, c * P : (c + 1) * P], False, c > 0)
+        for c in range(8 - TURNED, 8):
+            shifts[c] = shift(c, c - 8 + 2 * TURNED)
         pairs = sbuf([P, TURNED, 2, 2 * P], BF16, "pairs", "fresh10")
         for u in range(2):
-            nc.scalar.copy(out=pairs[:, 0:2, u, :].rearrange("j c (p e) -> j c p e", e=2), in_=pair_banks[u][:].rearrange("j c e p -> j c p e"))
-        nc.scalar.copy(out=pairs[:, 2, :, :].rearrange("j u (p e) -> j u p e", e=2), in_=third_bank[:].rearrange("j (u e) p -> j u p e", e=2))
+            nc.scalar.copy(out=pairs[:, 0:2, u, :].rearrange("j c (p e) -> j c p e", e=2),
+                           in_=pair_banks[u][:].rearrange("j c e p -> j c p e"))
+        nc.scalar.copy(out=pairs[:, 2, :, :].rearrange("j u (p e) -> j u p e", e=2),
+                       in_=third_bank[:].rearrange("j (u e) p -> j u p e", e=2))
         z_tiles = [sbuf([P, PIECE * PACK], BF16, "z%d" % q, tag) for q, tag in enumerate(("fresh12", "tab", "fresh01"))]
         for c in range(TURNED):
             words = bank(c, [P, 2, P], "words%d" % c)
@@ -304,20 +307,21 @@ def tile_list_tidal_pitch_features_kernel(tc, tab_words, tab_scales, offs, offs2
         def couple(c):
             nc.vector.tensor_tensor(
                 out=z_cols(c * P, (c + 1) * P).rearrange("p (c i t) -> p c t i", i=2, t=PACK),
-                in0=scaled[c // 4][:, :, (c % 4) * P : (c % 4 + 1) * P].rearrange("p t (c i) -> p c t i", i=2),
+                in0=scaled[:, :, c * P : (c + 1) * P].rearrange("p t (c i) -> p c t i", i=2),
                 in1=shifts[c][:].rearrange("p t (c i) -> p c t i", i=2), op=ALU.add)
 
-        def finish(lo, hi, banks, tag, last):
+        def finish(first, last, banks, tag, shared):
+            lo, hi = first * P, (last + 1) * P
             cols = slice(lo, hi)
             quantize(z_codes[:, cols], z_scales[:, cols], z_cols(lo, hi))
             result = sbuf([P, 2, hi - lo], F32, "result%d" % lo, tag)
-            for h in range(2):
+            for h in range(N // P):
                 y = bank(banks[h], [P, hi - lo], "y%d_%d" % (lo, h))
                 nc.tensor.matmul_mx(out=y[:], lhsT=wo_codes[:, P * h : P * (h + 1)].bitcast(FP8X4),
-                                    lhsT_scale=wo_plane[:, P * h : P * (h + 1)],
+                                    lhsT_scale=wo_block_scales[:, P * h : P * (h + 1)],
                                     rhs=z_codes[:, cols].bitcast(FP8X4), rhs_scale=z_scales[:, cols],
                                     start=True, stop=True)
-                if last and h == 1:
+                if shared and h == 1:
                     nc.vector.tensor_scalar(out=result[:, h, :], in0=y[:], scalar1=bo_cols[:, h : h + 1], scalar2=None, op0=ALU.add)
                 else:
                     nc.scalar.activation(out=result[:, h, :], in_=y[:], func=ACT.Identity, bias=bo_cols[:, h : h + 1])
@@ -329,10 +333,10 @@ def tile_list_tidal_pitch_features_kernel(tc, tab_words, tab_scales, offs, offs2
 
         for c in (3, 4, 5):
             couple(c)
-        finish(0, 256, (0, 6), "wp0_woven", False)
-        finish(512, 768, (1, 2), "wp1_woven", False)
+        finish(0, 1, (0, 6), "wp0_woven", False)
+        finish(4, 5, (1, 2), "wp1_woven", False)
         couple(6)
-        finish(256, 512, (7, 3), "wsh_woven", False)
+        finish(2, 3, (7, 3), "wsh_woven", False)
         couple(7)
-        finish(768, 896, (4, 1), "stage", True)
-        finish(896, 1024, (5, 2), "gain", True)
+        finish(6, 6, (4, 1), "plane10", True)
+        finish(7, 7, (5, 2), "gain", True)

@@ -231,10 +231,11 @@ def tile_list_tidal_pitch_features_kernel(tc, tab_words, tab_scales, offs, offs2
             wp_codes[1, t] = late_codes[:, P * t : P * (t + 1)]
         wsh_codes = late_codes[:, H : 2 * H]
         wsh_scales = sbuf([P, H], U8, "wsh_scales")
-        quantize(wsh_codes, wsh_scales[:], wsh_woven[:])
+        quantize(wsh_codes[:, 0 : H // 2], wsh_scales[:, 0 : H // 2], wsh_woven[:, 0 : H // 2 * PACK])
         proj = [sbuf([P, T], F32, "proj0", "plane00")]
         for acc, share in zip(first_accs, shares):
             (nc.vector.tensor_copy if share is shares[-1] else nc.scalar.copy)(out=proj[0][:, share[0][0] : share[-1][1]], in_=acc[:])
+        quantize(wsh_codes[:, H // 2 : H], wsh_scales[:, H // 2 : H], wsh_woven[:, H // 2 * PACK : H * PACK])
         for t in range(1, PACK):
             if t == 1:
                 proj.append(placed.tile([P, T], F32, name="proj1", offset=0, align_bytes=AL))
@@ -292,14 +293,17 @@ def tile_list_tidal_pitch_features_kernel(tc, tab_words, tab_scales, offs, offs2
                            in_=pair_banks[u][:].rearrange("j c e p -> j c p e"))
         nc.scalar.copy(out=pairs[:, 2, :, :].rearrange("j u (p e) -> j u p e", e=2),
                        in_=third_bank[:].rearrange("j (u e) p -> j u p e", e=2))
-        z_tiles = [sbuf([P, PIECE * PACK], BF16, "z%d" % q, tag) for q, tag in enumerate(("fresh12", "tab", "fresh01"))]
+        z_bytes = PIECE * PACK * 2
+        z_tiles = [placed.tile([P, PIECE * PACK], BF16, name="z0", offset=z_bytes // 2, align_bytes=AL),
+                   sbuf([P, PIECE * PACK], BF16, "z1", "tab"), sbuf([P, PIECE * PACK], BF16, "z2", "fresh01")]
         for c in range(TURNED):
             words = bank(c, [P, 2, P], "words%d" % c)
             for u in range(2):
                 nc.tensor.transpose(words[:, u, :], pairs[:, c, u, :].bitcast(F32), ident[:])
             nc.scalar.copy(out=z_tiles[c // 2][:].bitcast(F32).rearrange("p (c j u) -> p c j u", c=2, u=2)[:, c % 2, :, :],
                            in_=words[:].rearrange("p u j -> p j u"))
-        z_tiles.append(sbuf([P, PIECE * PACK], BF16, "z3", "fresh12"))
+        z_tiles.append(placed.tile([P, PIECE * PACK], BF16, name="z3", offset=z_bytes, align_bytes=AL))
+        held_codes = placed.tile([P, PIECE], U32, name="held_codes", offset=z_bytes // 4, align_bytes=AL)
 
         def z_cols(lo, hi):
             return z_tiles[lo // PIECE][:, lo % PIECE * PACK : (lo % PIECE + hi - lo) * PACK]
@@ -310,18 +314,19 @@ def tile_list_tidal_pitch_features_kernel(tc, tab_words, tab_scales, offs, offs2
                 in0=scaled[:, :, c * P : (c + 1) * P].rearrange("p t (c i) -> p c t i", i=2),
                 in1=shifts[c][:].rearrange("p t (c i) -> p c t i", i=2), op=ALU.add)
 
-        def finish(first, last, banks, tag, shared):
+        def finish(first, last, banks, tag, codes=None):
             lo, hi = first * P, (last + 1) * P
             cols = slice(lo, hi)
-            quantize(z_codes[:, cols], z_scales[:, cols], z_cols(lo, hi))
+            codes = z_codes[:, cols] if codes is None else codes
+            quantize(codes, z_scales[:, cols], z_cols(lo, hi))
             result = sbuf([P, 2, hi - lo], F32, "result%d" % lo, tag)
             for h in range(N // P):
                 y = bank(banks[h], [P, hi - lo], "y%d_%d" % (lo, h))
                 nc.tensor.matmul_mx(out=y[:], lhsT=wo_codes[:, P * h : P * (h + 1)].bitcast(FP8X4),
                                     lhsT_scale=wo_block_scales[:, P * h : P * (h + 1)],
-                                    rhs=z_codes[:, cols].bitcast(FP8X4), rhs_scale=z_scales[:, cols],
+                                    rhs=codes.bitcast(FP8X4), rhs_scale=z_scales[:, cols],
                                     start=True, stop=True)
-                if shared and h == 1:
+                if hi == S and h == 1:
                     nc.vector.tensor_scalar(out=result[:, h, :], in0=y[:], scalar1=bo_cols[:, h : h + 1], scalar2=None, op0=ALU.add)
                 else:
                     nc.scalar.activation(out=result[:, h, :], in_=y[:], func=ACT.Identity, bias=bo_cols[:, h : h + 1])
@@ -333,10 +338,10 @@ def tile_list_tidal_pitch_features_kernel(tc, tab_words, tab_scales, offs, offs2
 
         for c in (3, 4, 5):
             couple(c)
-        finish(0, 1, (0, 6), "wp0_woven", False)
-        finish(4, 5, (1, 2), "wp1_woven", False)
+        finish(0, 1, (0, 6), "wp0_woven")
+        finish(4, 5, (1, 2), "wp1_woven", held_codes[:])
         couple(6)
-        finish(2, 3, (7, 3), "wsh_woven", False)
+        finish(2, 3, (7, 3), "wsh_woven")
         couple(7)
-        finish(6, 6, (4, 1), "plane10", True)
-        finish(7, 7, (5, 2), "gain", True)
+        finish(6, 6, (4, 1), "plane10")
+        finish(7, 7, (5, 2), "gain")

@@ -32,7 +32,8 @@ ORDER = [(1, 2), (0, 0), (0, 1), (0, 2), (0, 3), (1, 0), (1, 1), (1, 3)]
 FIRST_PIECES = ((0, S // 4), (S // 4, S))
 CHUNKS = [(1536, 2048), (0, 512), (512, 1024), (1024, 1280), (1280, 1408), (1408, 1536)]
 BANK_ORDER = [3, 0, 1, 2]
-GPSIMD_RANGES = 3
+GPSIMD_CHUNKS = 2
+VECTOR_WEAVES = 384
 TURNED = 3
 PIECE = 2 * P
 
@@ -78,11 +79,9 @@ def tile_list_tidal_pitch_features_kernel(tc, tab_words, tab_scales, offs, offs2
         def gpsimd_copy(out, in_):
             nc.gpsimd.tensor_scalar(out=out, in0=in_, scalar1=1.0, scalar2=0.0, op0=ALU.mult, op1=ALU.add)
 
-        def weave_weight(engine_copy, raw, name, walk):
-            woven = sbuf([P, H * PACK], BF16, name)
-            engine_copy(out=woven[:].rearrange("p (t m j) -> " + walk, t=PACK, j=PACK),
+        def weave_weight(engine_copy, raw, woven, walk):
+            engine_copy(out=woven.rearrange("p t (m j) -> " + walk, j=PACK),
                         in_=raw[:].rearrange("p j (m t) -> " + walk, t=PACK))
-            return woven
 
         def quantize(codes, scales, woven):
             nc.vector.quantize_mx(out=codes.bitcast(FP8X4), scales=scales, in_=woven)
@@ -127,17 +126,17 @@ def tile_list_tidal_pitch_features_kernel(tc, tab_words, tab_scales, offs, offs2
 
         border = T * 4
         woven1 = {}
-        for lo, hi in CHUNKS[:-1]:
+        for lo, hi in CHUNKS[:-GPSIMD_CHUNKS]:
             woven1[lo] = sbuf([P, (hi - lo) * PACK], BF16, "woven1_%d" % lo)
-        lo, hi = CHUNKS[-1]
-        woven1[lo] = placed.tile([P, (hi - lo) * PACK], BF16, name="woven1_last", offset=border - (hi - lo) * PACK, align_bytes=AL)
 
-        def weave_plane(engine_copy, j, lo, hi):
-            engine_copy(out=woven1[lo][:].rearrange("p (c t) -> p c t", t=PACK)[:, :, j], in_=planes[1, j][:, lo:hi])
+        def weave_plane(engine_copy, j, lo, hi, first=None, last=None):
+            first, last = first or lo, last or hi
+            engine_copy(out=woven1[lo][:].rearrange("p (c t) -> p c t", t=PACK)[:, first - lo : last - lo, j],
+                        in_=planes[1, j][:, first:last])
 
         ident = sbuf([P, P], F32, "ident")
         make_identity(nc, ident[:])
-        stage = sbuf([P, PACK, T], BF16, "stage")
+        stage = placed.tile([P, PACK, T], BF16, name="stage", offset=border, align_bytes=AL)
 
         def stage_plane(j):
             nc.scalar.copy(out=stage[:, j, :], in_=planes[0, j][:])
@@ -151,7 +150,7 @@ def tile_list_tidal_pitch_features_kernel(tc, tab_words, tab_scales, offs, offs2
         lo, hi = CHUNKS[0]
         nc.scalar.copy(out=woven1[lo][:].rearrange("p (c t) -> p c t", t=PACK)[:, :, 2:4],
                        in_=planes[1, 2][:, lo:hi].unsqueeze(2).to_broadcast([P, hi - lo, 2]))
-        for lo, hi in CHUNKS[1:]:
+        for lo, hi in CHUNKS[1:-GPSIMD_CHUNKS]:
             weave_plane(nc.scalar.copy, 2, lo, hi)
         wsc_sorted = sbuf([P, 3 * H], U8, "wsc_sorted")
         nc.gpsimd.tensor_copy(out=wsc_sorted[:, 0 : 2 * H].rearrange("p (t m b) -> p t m b", t=PACK, b=2),
@@ -162,7 +161,8 @@ def tile_list_tidal_pitch_features_kernel(tc, tab_words, tab_scales, offs, offs2
         stage_plane(0)
         v_words = sbuf([P, S], U32, "v_words")
         nc.vector.tensor_copy(out=v_words[:], in_=tab[:].indirect(idx[:]))
-        wp_woven = [weave_weight(nc.scalar.copy, wp_raw[0], "wp0_woven", "p m j t")]
+        wp_woven = sbuf([P, PACK, 2, P * PACK], BF16, "wp_woven")
+        weave_weight(nc.scalar.copy, wp_raw[0], wp_woven[:, :, 0, :], "p m j t")
         gain = sbuf([P, PACK, S], F32, "gain")
         for t in range(PACK):
             for h in range(S // BANK):
@@ -175,44 +175,58 @@ def tile_list_tidal_pitch_features_kernel(tc, tab_words, tab_scales, offs, offs2
                 nc.scalar.activation(out=gain[:, t, cols], in_=sc[:], func=ACT.Exp, scale=amp_cols[:, t : t + 1])
         scatter((0, 1))
         stage_plane(1)
-        wp_woven.append(weave_weight(gpsimd_copy, wp_raw[1], "wp1_woven", "p t m j"))
+        weave_weight(gpsimd_copy, wp_raw[1], wp_woven[:, :, 1, :], "p t m j")
         scatter((0, 2))
         stage_plane(2)
-        wsh_woven = weave_weight(gpsimd_copy, wsh_raw, "wsh_woven", "p t m j")
+        wsh_blocks = sbuf([P, PACK, P * PACK], BF16, "wsh_woven")
+        weave_weight(gpsimd_copy, wsh_raw, wsh_blocks[:], "p t m j")
+        wsh_woven = wsh_blocks[:].rearrange("p t c -> p (t c)")
         scatter((0, 3))
         stage_plane(3)
         woven0 = [sbuf([P, HALF * PACK], BF16, "woven0_%d" % h, "wp%d_raw" % h) for h in range(2)]
-        for c in range(T // BANK):
-            (gpsimd_copy if c < GPSIMD_RANGES else nc.scalar.copy)(
+        for c in (2, 3, 0, 1):
+            gpsimd_copy(
                 out=woven0[c // 2][:, (c % 2) * BANK * PACK : (c % 2 + 1) * BANK * PACK].rearrange("p (c t) -> p c t", t=PACK),
                 in_=stage[:, :, c * BANK : (c + 1) * BANK].rearrange("p t c -> p c t"))
+        for (lo, hi), offset in zip(CHUNKS[-GPSIMD_CHUNKS:], (border + P * PACK, border - P * PACK)):
+            woven1[lo] = placed.tile([P, (hi - lo) * PACK], BF16, name="woven1_%d" % lo, offset=offset, align_bytes=AL)
+            gpsimd_copy(out=woven1[lo][:].rearrange("p (c t) -> p c t", t=PACK)[:, :, 2:4],
+                        in_=planes[1, 2][:, lo:hi].unsqueeze(2).to_broadcast([P, hi - lo, 2]))
         for j in range(2):
             scatter((1, j))
-            for lo, hi in CHUNKS:
-                weave_plane(nc.scalar.copy, j, lo, hi)
-        wp_scales = sbuf([P, 2, H], U8, "wp_scales")
-        early_codes = sbuf([P, H + P], U32, "early_codes", "fresh11")
-        quantize(early_codes[:, 0:H], wp_scales[:, 0, :], wp_woven[0][:])
-        quantize(early_codes[:, H : H + P], wp_scales[:, 1, 0:P], wp_woven[1][:, 0 : P * PACK])
+            for i, (lo, hi) in enumerate(CHUNKS):
+                weave_plane(nc.scalar.copy if i < len(CHUNKS) - GPSIMD_CHUNKS else gpsimd_copy, j, lo, hi)
         scatter((1, 3))
 
         page_scales = [sbuf([P, T], U8, "page_scales%d" % a) for a in range(2)]
-        page_codes = [sbuf([P, T], U32, "page_codes0", "fresh13"), sbuf([P, T], U32, "page_codes1", "wsh_raw")]
-        wp_codes = {(0, t): early_codes[:, P * t : P * (t + 1)] for t in range(PACK)}
-        wp_codes[1, 0] = early_codes[:, H : H + P]
+        early_codes = sbuf([P, T + 2 * P], U32, "early_codes", "fresh13")
+        page_codes = [early_codes[:, 0:T], sbuf([P, T], U32, "page_codes1", "wp0_raw")[:]]
+        wp_scales = sbuf([P, 2 * H], U8, "wp_scales")
+        wp_codes = {}
+
+        def quantize_wp(codes, first, last):
+            quantize(codes, wp_scales[:, 2 * first * P : 2 * last * P],
+                     wp_woven[:, first:last, :, :].rearrange("p t a c -> p (t a c)"))
+            for b in range(2 * first, 2 * last):
+                wp_codes[b % 2, b // 2] = codes[:, (b - 2 * first) * P : (b - 2 * first + 1) * P]
+
+        quantize_wp(early_codes[:, T : T + 2 * P], 0, 1)
 
         def quantize_page(a, lo, hi, woven):
             quantize(page_codes[a][:, lo:hi], page_scales[a][:, lo:hi], woven)
 
         def page_pass(acc, t, a, lo, hi, start, stop):
             nc.tensor.matmul_mx(out=acc, lhsT=wp_codes[a, t].bitcast(FP8X4),
-                                lhsT_scale=wp_scales[:, a, P * t : P * (t + 1)],
+                                lhsT_scale=wp_scales[:, P * (2 * t + a) : P * (2 * t + a + 1)],
                                 rhs=page_codes[a][:, lo:hi].bitcast(FP8X4), rhs_scale=page_scales[a][:, lo:hi],
                                 start=start, stop=stop)
 
         quantize_page(0, HALF, T, woven0[1][:])
-        for i, (lo, hi) in enumerate(CHUNKS):
-            weave_plane(nc.vector.tensor_copy if i == 0 else nc.scalar.copy, 3, lo, hi)
+        lo, hi = CHUNKS[0]
+        weave_plane(nc.vector.tensor_copy, 3, lo, hi, lo, lo + VECTOR_WEAVES)
+        weave_plane(nc.scalar.copy, 3, lo, hi, lo + VECTOR_WEAVES, hi)
+        for lo, hi in CHUNKS[1:]:
+            weave_plane(nc.scalar.copy, 3, lo, hi)
         quantize_page(0, 0, HALF, woven0[0][:])
         shares = [CHUNKS[0:1], CHUNKS[1:2], CHUNKS[2:3], CHUNKS[3:5], CHUNKS[5:6]]
         first_accs = [bank(b, [P, share[-1][1] - share[0][0]], "acc0_%d" % b) for b, share in zip((0, 1, 2, 3, 7), shares)]
@@ -224,12 +238,10 @@ def tile_list_tidal_pitch_features_kernel(tc, tab_words, tab_scales, offs, offs2
             for lo, hi in share:
                 quantize_page(1, lo, hi, woven1[lo][:])
                 page_pass(acc[:, lo - share[0][0] : hi - share[0][0]], 0, 1, lo, hi, False, hi == share[-1][1])
-        late_codes = placed.tile([P, 2 * H], U32, name="late_codes", offset=border, align_bytes=AL)
-        for lo, hi in ((P, 2 * P), (2 * P, H)):
-            quantize(late_codes[:, lo:hi], wp_scales[:, 1, lo:hi], wp_woven[1][:, lo * PACK : hi * PACK])
-        for t in range(1, PACK):
-            wp_codes[1, t] = late_codes[:, P * t : P * (t + 1)]
-        wsh_codes = late_codes[:, H : 2 * H]
+        late_codes = placed.tile([P, 6 * P + H], U32, name="late_codes", offset=border, align_bytes=AL)
+        quantize_wp(late_codes[:, 0 : 2 * P], 1, 2)
+        quantize_wp(late_codes[:, 2 * P : 6 * P], 2, 4)
+        wsh_codes = late_codes[:, 6 * P : 6 * P + H]
         wsh_scales = sbuf([P, H], U8, "wsh_scales")
         quantize(wsh_codes[:, 0 : H // 2], wsh_scales[:, 0 : H // 2], wsh_woven[:, 0 : H // 2 * PACK])
         proj = [sbuf([P, T], F32, "proj0", "plane00")]
@@ -247,7 +259,7 @@ def tile_list_tidal_pitch_features_kernel(tc, tab_words, tab_scales, offs, offs2
                     page_pass(acc[:], t, a, c * BANK, (c + 1) * BANK, a == 0, a == 1)
                 nc.scalar.copy(out=proj[t][:, c * BANK : (c + 1) * BANK], in_=acc[:])
 
-        scaled = sbuf([P, PACK, S], F32, "scaled", "stage")
+        scaled = placed.tile([P, PACK, S], F32, name="scaled", offset=border + (6 * P + H) * 4, align_bytes=AL)
         for t in range(PACK):
             for lo, hi in ((0, S),) if t < PACK - 1 else ((0, S // 2), (S // 2, S)):
                 nc.vector.tensor_tensor(out=scaled[:, t, lo:hi], in0=proj[t][:].indirect(idx3[:, lo // GROUP : hi // GROUP]),
@@ -338,8 +350,8 @@ def tile_list_tidal_pitch_features_kernel(tc, tab_words, tab_scales, offs, offs2
 
         for c in (3, 4, 5):
             couple(c)
-        finish(0, 1, (0, 6), "wp0_woven")
-        finish(4, 5, (1, 2), "wp1_woven", held_codes[:])
+        finish(0, 1, (0, 6), "wp_woven")
+        finish(4, 5, (1, 2), "plane11", held_codes[:])
         couple(6)
         finish(2, 3, (7, 3), "wsh_woven")
         couple(7)

@@ -33,7 +33,7 @@ FIRST_PIECES = ((0, S // 4), (S // 4, S))
 CHUNKS = [(1536, 2048), (0, 512), (512, 1024), (1024, 1280), (1280, 1408), (1408, 1536)]
 BANK_ORDER = [3, 0, 1, 2]
 GPSIMD_CHUNKS = 2
-VECTOR_WEAVES = 384
+VECTOR_WEAVES = 416
 TURNED = 3
 PIECE = 2 * P
 
@@ -93,6 +93,8 @@ def tile_list_tidal_pitch_features_kernel(tc, tab_words, tab_scales, offs, offs2
         nc.gpsimd.memset(tab_rows[0 : P - SCALE_ROWS, :].bitcast(I32), 0)
         nc.sync.dma_start(out=tab_rows[P - SCALE_ROWS : P, :].bitcast(I32), in_=tab_scales[0].bitcast(I32))
         nc.sync.dma_start(out=idx[:], in_=offs)
+        tab = sbuf([P, T], U32, "tab")
+        nc.sync.dma_start(out=tab[:].bitcast(I32), in_=tab_words[0].rearrange("p t i -> p (t i)").bitcast(I32))
         nc.sync.dma_start(out=idx2[:], in_=offs2)
         load_plane(ORDER[0], FIRST_PIECES)
 
@@ -107,8 +109,6 @@ def tile_list_tidal_pitch_features_kernel(tc, tab_words, tab_scales, offs, offs2
         nc.sync.dma_start(out=wsc_raw[:].bitcast(I32), in_=wsc_words[0].bitcast(I32))
         move_scale_rows(nc.sync, wsc_raw_scales, wsc_scales[0])
         nc.sync.dma_start(out=amp_cols[:], in_=amp.rearrange("(p t) -> p t", t=PACK))
-        tab = sbuf([P, T], U32, "tab")
-        nc.sync.dma_start(out=tab[:].bitcast(I32), in_=tab_words[0].rearrange("p t i -> p (t i)").bitcast(I32))
         wp_raw = [load_weight(wp[0:H, :], "wp0_raw")]
         load_plane(ORDER[2])
         wp_raw.append(load_weight(wp[H : 2 * H, :], "wp1_raw"))
@@ -146,6 +146,8 @@ def tile_list_tidal_pitch_features_kernel(tc, tab_words, tab_scales, offs, offs2
         v_scales = sbuf([P, S], U8, "v_scales")
         nc.gpsimd.memset(v_scales[:].bitcast(I32), 0)
         move_scale_rows(nc.scalar, v_scales, v_rows[P - SCALE_ROWS : P, :])
+        v_words = sbuf([P, S], U32, "v_words")
+        nc.vector.tensor_copy(out=v_words[:], in_=tab[:].indirect(idx[:]))
         scatter((1, 2), FIRST_PIECES)
         lo, hi = CHUNKS[0]
         nc.scalar.copy(out=woven1[lo][:].rearrange("p (c t) -> p c t", t=PACK)[:, :, 2:4],
@@ -159,9 +161,8 @@ def tile_list_tidal_pitch_features_kernel(tc, tab_words, tab_scales, offs, offs2
                               in_=wsc_raw_scales[:].rearrange("p (m t) -> p t m", t=PACK))
         scatter((0, 0))
         stage_plane(0)
-        v_words = sbuf([P, S], U32, "v_words")
-        nc.vector.tensor_copy(out=v_words[:], in_=tab[:].indirect(idx[:]))
-        wp_woven = sbuf([P, PACK, 2, P * PACK], BF16, "wp_woven")
+        weights = sbuf([P, 3 * PACK, P * PACK], BF16, "weights")
+        wp_woven = weights[:, 0 : 2 * PACK, :].rearrange("p (t a) c -> p t a c", a=2)
         weave_weight(nc.scalar.copy, wp_raw[0], wp_woven[:, :, 0, :], "p m j t")
         gain = sbuf([P, PACK, S], F32, "gain")
         for t in range(PACK):
@@ -178,9 +179,7 @@ def tile_list_tidal_pitch_features_kernel(tc, tab_words, tab_scales, offs, offs2
         weave_weight(gpsimd_copy, wp_raw[1], wp_woven[:, :, 1, :], "p t m j")
         scatter((0, 2))
         stage_plane(2)
-        wsh_blocks = sbuf([P, PACK, P * PACK], BF16, "wsh_woven")
-        weave_weight(gpsimd_copy, wsh_raw, wsh_blocks[:], "p t m j")
-        wsh_woven = wsh_blocks[:].rearrange("p t c -> p (t c)")
+        weave_weight(gpsimd_copy, wsh_raw, weights[:, 2 * PACK : 3 * PACK, :], "p t m j")
         scatter((0, 3))
         stage_plane(3)
         woven0 = [sbuf([P, HALF * PACK], BF16, "woven0_%d" % h, "wp%d_raw" % h) for h in range(2)]
@@ -201,23 +200,22 @@ def tile_list_tidal_pitch_features_kernel(tc, tab_words, tab_scales, offs, offs2
         page_scales = [sbuf([P, T], U8, "page_scales%d" % a) for a in range(2)]
         early_codes = sbuf([P, T + 2 * P], U32, "early_codes", "fresh13")
         page_codes = [early_codes[:, 0:T], sbuf([P, T], U32, "page_codes1", "wp0_raw")[:]]
-        wp_scales = sbuf([P, 2 * H], U8, "wp_scales")
-        wp_codes = {}
+        weight_scales = sbuf([P, 3 * H], U8, "weight_scales")
+        weight_codes = {}
 
-        def quantize_wp(codes, first, last):
-            quantize(codes, wp_scales[:, 2 * first * P : 2 * last * P],
-                     wp_woven[:, first:last, :, :].rearrange("p t a c -> p (t a c)"))
-            for b in range(2 * first, 2 * last):
-                wp_codes[b % 2, b // 2] = codes[:, (b - 2 * first) * P : (b - 2 * first + 1) * P]
+        def quantize_weights(codes, first, last):
+            quantize(codes, weight_scales[:, first * P : last * P], weights[:, first:last, :].rearrange("p b c -> p (b c)"))
+            for b in range(first, last):
+                weight_codes[b] = codes[:, (b - first) * P : (b - first + 1) * P]
 
-        quantize_wp(early_codes[:, T : T + 2 * P], 0, 1)
+        quantize_weights(early_codes[:, T : T + 2 * P], 0, 2)
 
         def quantize_page(a, lo, hi, woven):
             quantize(page_codes[a][:, lo:hi], page_scales[a][:, lo:hi], woven)
 
         def page_pass(acc, t, a, lo, hi, start, stop):
-            nc.tensor.matmul_mx(out=acc, lhsT=wp_codes[a, t].bitcast(FP8X4),
-                                lhsT_scale=wp_scales[:, P * (2 * t + a) : P * (2 * t + a + 1)],
+            nc.tensor.matmul_mx(out=acc, lhsT=weight_codes[2 * t + a].bitcast(FP8X4),
+                                lhsT_scale=weight_scales[:, P * (2 * t + a) : P * (2 * t + a + 1)],
                                 rhs=page_codes[a][:, lo:hi].bitcast(FP8X4), rhs_scale=page_scales[a][:, lo:hi],
                                 start=start, stop=stop)
 
@@ -239,15 +237,11 @@ def tile_list_tidal_pitch_features_kernel(tc, tab_words, tab_scales, offs, offs2
                 quantize_page(1, lo, hi, woven1[lo][:])
                 page_pass(acc[:, lo - share[0][0] : hi - share[0][0]], 0, 1, lo, hi, False, hi == share[-1][1])
         late_codes = placed.tile([P, 6 * P + H], U32, name="late_codes", offset=border, align_bytes=AL)
-        quantize_wp(late_codes[:, 0 : 2 * P], 1, 2)
-        quantize_wp(late_codes[:, 2 * P : 6 * P], 2, 4)
-        wsh_codes = late_codes[:, 6 * P : 6 * P + H]
-        wsh_scales = sbuf([P, H], U8, "wsh_scales")
-        quantize(wsh_codes[:, 0 : H // 2], wsh_scales[:, 0 : H // 2], wsh_woven[:, 0 : H // 2 * PACK])
+        quantize_weights(late_codes[:, 0 : 2 * P], 2, 4)
         proj = [sbuf([P, T], F32, "proj0", "plane00")]
         for acc, share in zip(first_accs, shares):
             (nc.vector.tensor_copy if share is shares[-1] else nc.scalar.copy)(out=proj[0][:, share[0][0] : share[-1][1]], in_=acc[:])
-        quantize(wsh_codes[:, H // 2 : H], wsh_scales[:, H // 2 : H], wsh_woven[:, H // 2 * PACK : H * PACK])
+        quantize_weights(late_codes[:, 2 * P : 10 * P], 4, 12)
         for t in range(1, PACK):
             if t == 1:
                 proj.append(placed.tile([P, T], F32, name="proj1", offset=0, align_bytes=AL))
@@ -272,8 +266,8 @@ def tile_list_tidal_pitch_features_kernel(tc, tab_words, tab_scales, offs, offs2
             sh = bank(b, [P, PACK, P], "sh%d" % c)
             cols = slice(c * P, (c + 1) * P)
             for t in range(PACK):
-                nc.tensor.matmul_mx(out=sh[:, t, :], lhsT=wsh_codes[:, P * t : P * (t + 1)].bitcast(FP8X4),
-                                    lhsT_scale=wsh_scales[:, P * t : P * (t + 1)],
+                nc.tensor.matmul_mx(out=sh[:, t, :], lhsT=weight_codes[8 + t].bitcast(FP8X4),
+                                    lhsT_scale=weight_scales[:, P * (8 + t) : P * (9 + t)],
                                     rhs=v_words[:, cols].bitcast(FP8X4), rhs_scale=v_scales[:, cols],
                                     start=True, stop=True)
             return sh
@@ -350,10 +344,10 @@ def tile_list_tidal_pitch_features_kernel(tc, tab_words, tab_scales, offs, offs2
 
         for c in (3, 4, 5):
             couple(c)
-        finish(0, 1, (0, 6), "wp_woven")
+        finish(0, 1, (0, 6), "weights")
         finish(4, 5, (1, 2), "plane11", held_codes[:])
         couple(6)
-        finish(2, 3, (7, 3), "wsh_woven")
+        finish(2, 3, (7, 3), "wsh_raw")
         couple(7)
         finish(6, 6, (4, 1), "plane10")
         finish(7, 7, (5, 2), "gain")

@@ -176,17 +176,16 @@ def tile_list_tidal_pitch_features_kernel(tc, tab_words, tab_scales, offs, offs2
                 nc.scalar.activation(out=gain[:, t, cols], in_=sc[:], func=ACT.Exp, scale=amp_cols[:, t : t + 1])
         scatter((0, 1))
         stage_plane(1)
-        weave_weight(gpsimd_copy, wp_raw[1], wp_woven[:, :, 1, :], "p t m j")
+        weave_weight(nc.scalar.copy, wp_raw[1], wp_woven[:, :, 1, :], "p m j t")
         scatter((0, 2))
         stage_plane(2)
-        weave_weight(gpsimd_copy, wsh_raw, weights[:, 2 * PACK : 3 * PACK, :], "p t m j")
+        weave_weight(nc.scalar.copy, wsh_raw, weights[:, 2 * PACK : 3 * PACK, :], "p m j t")
         scatter((0, 3))
         stage_plane(3)
         woven0 = [sbuf([P, HALF * PACK], BF16, "woven0_%d" % h, "wp%d_raw" % h) for h in range(2)]
-        for c in (2, 3, 0, 1):
-            gpsimd_copy(
-                out=woven0[c // 2][:, (c % 2) * BANK * PACK : (c % 2 + 1) * BANK * PACK].rearrange("p (c t) -> p c t", t=PACK),
-                in_=stage[:, :, c * BANK : (c + 1) * BANK].rearrange("p t c -> p c t"))
+        for lo, hi in ((HALF, T - P), (0, HALF), (T - P, T)):
+            gpsimd_copy(out=woven0[lo // HALF][:, lo % HALF * PACK : (lo % HALF + hi - lo) * PACK].rearrange("p (c t) -> p c t", t=PACK),
+                        in_=stage[:, :, lo:hi].rearrange("p t c -> p c t"))
         for (lo, hi), offset in zip(CHUNKS[-GPSIMD_CHUNKS:], (border + P * PACK, border - P * PACK)):
             woven1[lo] = placed.tile([P, (hi - lo) * PACK], BF16, name="woven1_%d" % lo, offset=offset, align_bytes=AL)
             gpsimd_copy(out=woven1[lo][:].rearrange("p (c t) -> p c t", t=PACK)[:, :, 2:4],
@@ -219,16 +218,16 @@ def tile_list_tidal_pitch_features_kernel(tc, tab_words, tab_scales, offs, offs2
                                 rhs=page_codes[a][:, lo:hi].bitcast(FP8X4), rhs_scale=page_scales[a][:, lo:hi],
                                 start=start, stop=stop)
 
-        quantize_page(0, HALF, T, woven0[1][:])
+        quantize_page(0, 0, HALF, woven0[0][:])
         lo, hi = CHUNKS[0]
         weave_plane(nc.vector.tensor_copy, 3, lo, hi, lo, lo + VECTOR_WEAVES)
         weave_plane(nc.scalar.copy, 3, lo, hi, lo + VECTOR_WEAVES, hi)
         for lo, hi in CHUNKS[1:]:
             weave_plane(nc.scalar.copy, 3, lo, hi)
-        quantize_page(0, 0, HALF, woven0[0][:])
+        quantize_page(0, HALF, T, woven0[1][:])
         shares = [CHUNKS[0:1], CHUNKS[1:2], CHUNKS[2:3], CHUNKS[3:5], CHUNKS[5:6]]
         first_accs = [bank(b, [P, share[-1][1] - share[0][0]], "acc0_%d" % b) for b, share in zip((0, 1, 2, 3, 7), shares)]
-        upper_half_first = sorted(zip(first_accs, shares), key=lambda pair: pair[1][0][0] < HALF)
+        upper_half_first = sorted(zip(first_accs, shares), key=lambda pair: pair[1][0][0] >= HALF)
         for acc, share in upper_half_first:
             for lo, hi in share:
                 page_pass(acc[:, lo - share[0][0] : hi - share[0][0]], 0, 0, lo, hi, lo == share[0][0], False)
@@ -332,7 +331,7 @@ def tile_list_tidal_pitch_features_kernel(tc, tab_words, tab_scales, offs, offs2
                                     lhsT_scale=wo_block_scales[:, P * h : P * (h + 1)],
                                     rhs=codes.bitcast(FP8X4), rhs_scale=z_scales[:, cols],
                                     start=True, stop=True)
-                if hi == S and h == 1:
+                if first == last and h == 1:
                     nc.vector.tensor_scalar(out=result[:, h, :], in0=y[:], scalar1=bo_cols[:, h : h + 1], scalar2=None, op0=ALU.add)
                 else:
                     nc.scalar.activation(out=result[:, h, :], in_=y[:], func=ACT.Identity, bias=bo_cols[:, h : h + 1])
@@ -345,9 +344,9 @@ def tile_list_tidal_pitch_features_kernel(tc, tab_words, tab_scales, offs, offs2
         for c in (3, 4, 5):
             couple(c)
         finish(0, 1, (0, 6), "weights")
+        finish(2, 3, (7, 3), "wsh_raw")
         finish(4, 5, (1, 2), "plane11", held_codes[:])
         couple(6)
-        finish(2, 3, (7, 3), "wsh_raw")
         couple(7)
-        finish(6, 6, (4, 1), "plane10")
-        finish(7, 7, (5, 2), "gain")
+        finish(6, 6, (4, 0), "plane10")
+        finish(7, 7, (5, 6), "gain")

@@ -253,10 +253,15 @@ def tile_list_tidal_pitch_features_kernel(tc, tab_words, tab_scales, offs, offs2
                 nc.scalar.copy(out=proj[t][:, c * BANK : (c + 1) * BANK], in_=acc[:])
 
         scaled = placed.tile([P, PACK, S], F32, name="scaled", offset=border + (6 * P + H) * 4, align_bytes=AL)
-        for t in range(PACK):
-            for lo, hi in ((0, S),) if t < PACK - 1 else ((0, S // 2), (S // 2, S)):
-                nc.vector.tensor_tensor(out=scaled[:, t, lo:hi], in0=proj[t][:].indirect(idx3[:, lo // GROUP : hi // GROUP]),
-                                        in1=gain[:, t, lo:hi], op=ALU.mult)
+
+        def gather(t, lo, hi):
+            nc.vector.tensor_tensor(out=scaled[:, t, lo:hi], in0=proj[t][:].indirect(idx3[:, lo // GROUP : hi // GROUP]),
+                                    in1=gain[:, t, lo:hi], op=ALU.mult)
+
+        for t in range(PACK - 1):
+            gather(t, 0, S)
+        gather(PACK - 1, 0, 2 * P)
+        gather(PACK - 1, 2 * P, 5 * P)
         z_codes = sbuf([P, S], U32, "z_codes", "fresh00")
         z_scales = sbuf([P, S], U8, "z_scales")
         out_rows = out.rearrange("(h p) j -> p h j", p=P)
@@ -271,10 +276,10 @@ def tile_list_tidal_pitch_features_kernel(tc, tab_words, tab_scales, offs, offs2
                                     start=True, stop=True)
             return sh
 
-        shifts = {c: shift(c, TURNED + c) for c in range(8 - TURNED)}
+        shifts = {c: shift(c, b) for c, b in ((0, 0), (2, 1), (1, 2), (3, 3), (4, 4))}
         shift_sbuf = sbuf([P, TURNED, PACK, P], F32, "shift_sbuf", "plane12")
-        pair_banks = [bank(u, [P, 2, 2, P], "turned%d" % u) for u in range(2)]
-        third_bank = bank(2, [P, PACK, P], "turned2")
+        pair_banks = [bank(5 + u, [P, 2, 2, P], "turned%d" % u) for u in range(2)]
+        third_bank = bank(7, [P, PACK, P], "turned2")
 
         def turn(c, t, src, start, stop):
             acc = pair_banks[t // 2][:, c, t % 2, :] if c < 2 else third_bank[:, t, :]
@@ -283,15 +288,15 @@ def tile_list_tidal_pitch_features_kernel(tc, tab_words, tab_scales, offs, offs2
         opens_a_bank = ((0, 0), (0, 2), (2, 0))
         for t in range(PACK - 1):
             for c in range(TURNED):
-                turn(c, t, scaled[:, t, c * P : (c + 1) * P], (c, t) in opens_a_bank, False)
+                turn(c, t, scaled[:, t, (2 + c) * P : (3 + c) * P], (c, t) in opens_a_bank, False)
         for c in range(TURNED):
-            nc.scalar.copy(out=shift_sbuf[:, c, :, :], in_=shifts[c][:])
+            nc.scalar.copy(out=shift_sbuf[:, c, :, :], in_=shifts[2 + c][:])
         for c, t in [(c, t) for t in range(PACK) for c in range(2)] + [(2, t) for t in range(PACK)]:
             turn(c, t, shift_sbuf[:, c, t, :], False, (c, t) == (1, 1))
         for c in range(TURNED):
-            turn(c, PACK - 1, scaled[:, PACK - 1, c * P : (c + 1) * P], False, c > 0)
-        for c in range(8 - TURNED, 8):
-            shifts[c] = shift(c, c - 8 + 2 * TURNED)
+            turn(c, PACK - 1, scaled[:, PACK - 1, (2 + c) * P : (3 + c) * P], False, c > 0)
+        for c, b in ((5, 1), (6, 3), (7, 4)):
+            shifts[c] = shift(c, b)
         pairs = sbuf([P, TURNED, 2, 2 * P], BF16, "pairs", "fresh10")
         for u in range(2):
             nc.scalar.copy(out=pairs[:, 0:2, u, :].rearrange("j c (p e) -> j c p e", e=2),
@@ -299,19 +304,20 @@ def tile_list_tidal_pitch_features_kernel(tc, tab_words, tab_scales, offs, offs2
         nc.scalar.copy(out=pairs[:, 2, :, :].rearrange("j u (p e) -> j u p e", e=2),
                        in_=third_bank[:].rearrange("j (u e) p -> j u p e", e=2))
         z_bytes = PIECE * PACK * 2
-        z_tiles = [placed.tile([P, PIECE * PACK], BF16, name="z0", offset=z_bytes // 2, align_bytes=AL),
-                   sbuf([P, PIECE * PACK], BF16, "z1", "tab"), sbuf([P, PIECE * PACK], BF16, "z2", "fresh01")]
-        for c in range(TURNED):
-            words = bank(c, [P, 2, P], "words%d" % c)
-            for u in range(2):
-                nc.tensor.transpose(words[:, u, :], pairs[:, c, u, :].bitcast(F32), ident[:])
-            nc.scalar.copy(out=z_tiles[c // 2][:].bitcast(F32).rearrange("p (c j u) -> p c j u", c=2, u=2)[:, c % 2, :, :],
-                           in_=words[:].rearrange("p u j -> p j u"))
-        z_tiles.append(placed.tile([P, PIECE * PACK], BF16, name="z3", offset=z_bytes, align_bytes=AL))
-        held_codes = placed.tile([P, PIECE], U32, name="held_codes", offset=z_bytes // 4, align_bytes=AL)
+        z_tiles = [sbuf([P, PIECE * PACK], BF16, "z0", "tab"),
+                   placed.tile([P, PIECE * PACK], BF16, name="z1", offset=0, align_bytes=AL),
+                   sbuf([P, PIECE * PACK], BF16, "z2", "fresh01")]
 
         def z_cols(lo, hi):
             return z_tiles[lo // PIECE][:, lo % PIECE * PACK : (lo % PIECE + hi - lo) * PACK]
+
+        for c in range(TURNED):
+            words = bank(5 + c, [P, 2, P], "words%d" % c)
+            for u in range(2):
+                nc.tensor.transpose(words[:, u, :], pairs[:, c, u, :].bitcast(F32), ident[:])
+            nc.scalar.copy(out=z_cols((2 + c) * P, (3 + c) * P).bitcast(F32).rearrange("p (j u) -> p j u", u=2),
+                           in_=words[:].rearrange("p u j -> p j u"))
+        z_tiles.append(placed.tile([P, PIECE * PACK], BF16, name="z3", offset=z_bytes // 2, align_bytes=AL))
 
         def couple(c):
             nc.vector.tensor_tensor(
@@ -319,10 +325,10 @@ def tile_list_tidal_pitch_features_kernel(tc, tab_words, tab_scales, offs, offs2
                 in0=scaled[:, :, c * P : (c + 1) * P].rearrange("p t (c i) -> p c t i", i=2),
                 in1=shifts[c][:].rearrange("p t (c i) -> p c t i", i=2), op=ALU.add)
 
-        def finish(first, last, banks, tag, codes=None):
+        def finish(first, last, banks, tag):
             lo, hi = first * P, (last + 1) * P
             cols = slice(lo, hi)
-            codes = z_codes[:, cols] if codes is None else codes
+            codes = z_codes[:, cols]
             quantize(codes, z_scales[:, cols], z_cols(lo, hi))
             result = sbuf([P, 2, hi - lo], F32, "result%d" % lo, tag)
             for h in range(N // P):
@@ -341,12 +347,14 @@ def tile_list_tidal_pitch_features_kernel(tc, tab_words, tab_scales, offs, offs2
             else:
                 nc.sync.dma_start(out=out_rows[:, :, cols], in_=result[:])
 
-        for c in (3, 4, 5):
-            couple(c)
-        finish(0, 1, (0, 6), "weights")
-        finish(2, 3, (7, 3), "wsh_raw")
-        finish(4, 5, (1, 2), "plane11", held_codes[:])
+        couple(0)
+        couple(1)
+        gather(PACK - 1, 5 * P, S)
+        finish(0, 1, (0, 2), "weights")
+        couple(5)
+        finish(2, 3, (5, 6), "wsh_raw")
+        finish(4, 5, (7, 1), "plane11")
         couple(6)
         couple(7)
-        finish(6, 6, (4, 0), "plane10")
-        finish(7, 7, (5, 6), "gain")
+        finish(6, 6, (3, 0), "plane10")
+        finish(7, 7, (4, 2), "gain")

@@ -30,10 +30,10 @@ AL = 64
 
 ORDER = [(1, 2), (0, 0), (0, 1), (0, 2), (0, 3), (1, 0), (1, 1), (1, 3)]
 FIRST_PIECES = ((0, S // 4), (S // 4, S))
-CHUNKS = [(1536, 2048), (0, 512), (512, 1024), (1024, 1280), (1280, 1408), (1408, 1536)]
+CHUNKS = [(1536, 2048), (0, 512), (512, 1024), (1024, 1280), (1280, 1536)]
 BANK_ORDER = [3, 0, 1, 2]
-GPSIMD_CHUNKS = 2
-VECTOR_WEAVES = 416
+GPSIMD_CHUNKS = 1
+VECTOR_WEAVES = 512
 TURNED = 3
 PIECE = 2 * P
 
@@ -186,7 +186,7 @@ def tile_list_tidal_pitch_features_kernel(tc, tab_words, tab_scales, offs, offs2
         for lo, hi in ((HALF, T - P), (0, HALF), (T - P, T)):
             gpsimd_copy(out=woven0[lo // HALF][:, lo % HALF * PACK : (lo % HALF + hi - lo) * PACK].rearrange("p (c t) -> p c t", t=PACK),
                         in_=stage[:, :, lo:hi].rearrange("p t c -> p c t"))
-        for (lo, hi), offset in zip(CHUNKS[-GPSIMD_CHUNKS:], (border + P * PACK, border - P * PACK)):
+        for (lo, hi), offset in zip(CHUNKS[-GPSIMD_CHUNKS:], (border - 2 * P * PACK,)):
             woven1[lo] = placed.tile([P, (hi - lo) * PACK], BF16, name="woven1_%d" % lo, offset=offset, align_bytes=AL)
             gpsimd_copy(out=woven1[lo][:].rearrange("p (c t) -> p c t", t=PACK)[:, :, 2:4],
                         in_=planes[1, 2][:, lo:hi].unsqueeze(2).to_broadcast([P, hi - lo, 2]))
@@ -221,12 +221,11 @@ def tile_list_tidal_pitch_features_kernel(tc, tab_words, tab_scales, offs, offs2
         quantize_page(0, 0, HALF, woven0[0][:])
         lo, hi = CHUNKS[0]
         weave_plane(nc.vector.tensor_copy, 3, lo, hi, lo, lo + VECTOR_WEAVES)
-        weave_plane(nc.scalar.copy, 3, lo, hi, lo + VECTOR_WEAVES, hi)
         for lo, hi in CHUNKS[1:]:
             weave_plane(nc.scalar.copy, 3, lo, hi)
         quantize_page(0, HALF, T, woven0[1][:])
-        shares = [CHUNKS[0:1], CHUNKS[1:2], CHUNKS[2:3], CHUNKS[3:5], CHUNKS[5:6]]
-        first_accs = [bank(b, [P, share[-1][1] - share[0][0]], "acc0_%d" % b) for b, share in zip((0, 1, 2, 3, 7), shares)]
+        shares = [CHUNKS[0:1], CHUNKS[1:2], CHUNKS[2:3], CHUNKS[3:5]]
+        first_accs = [bank(b, [P, share[-1][1] - share[0][0]], "acc0_%d" % b) for b, share in enumerate(shares)]
         upper_half_first = sorted(zip(first_accs, shares), key=lambda pair: pair[1][0][0] >= HALF)
         for acc, share in upper_half_first:
             for lo, hi in share:
@@ -239,7 +238,7 @@ def tile_list_tidal_pitch_features_kernel(tc, tab_words, tab_scales, offs, offs2
         quantize_weights(late_codes[:, 0 : 2 * P], 2, 4)
         proj = [sbuf([P, T], F32, "proj0", "plane00")]
         for acc, share in zip(first_accs, shares):
-            (nc.vector.tensor_copy if share is shares[-1] else nc.scalar.copy)(out=proj[0][:, share[0][0] : share[-1][1]], in_=acc[:])
+            nc.scalar.copy(out=proj[0][:, share[0][0] : share[-1][1]], in_=acc[:])
         quantize_weights(late_codes[:, 2 * P : 10 * P], 4, 12)
         for t in range(1, PACK):
             if t == 1:

@@ -93,10 +93,10 @@ def tile_list_tidal_pitch_features_kernel(tc, tab_words, tab_scales, offs, offs2
         nc.gpsimd.memset(tab_rows[0 : P - SCALE_ROWS, :].bitcast(I32), 0)
         nc.sync.dma_start(out=tab_rows[P - SCALE_ROWS : P, :].bitcast(I32), in_=tab_scales[0].bitcast(I32))
         nc.sync.dma_start(out=idx[:], in_=offs)
-        tab = sbuf([P, T], U32, "tab")
-        nc.sync.dma_start(out=tab[:].bitcast(I32), in_=tab_words[0].rearrange("p t i -> p (t i)").bitcast(I32))
         nc.sync.dma_start(out=idx2[:], in_=offs2)
         load_plane(ORDER[0], FIRST_PIECES)
+        tab = sbuf([P, T], U32, "tab")
+        nc.sync.dma_start(out=tab[:].bitcast(I32), in_=tab_words[0].rearrange("p t i -> p (t i)").bitcast(I32))
 
         wsc_raw = sbuf([P, 2 * H], U8, "wsc_raw")
         wsc_raw_scales = sbuf([P, H], U8, "wsc_raw_scales")
@@ -147,8 +147,8 @@ def tile_list_tidal_pitch_features_kernel(tc, tab_words, tab_scales, offs, offs2
         nc.gpsimd.memset(v_scales[:].bitcast(I32), 0)
         move_scale_rows(nc.scalar, v_scales, v_rows[P - SCALE_ROWS : P, :])
         v_words = sbuf([P, S], U32, "v_words")
-        nc.vector.tensor_copy(out=v_words[:], in_=tab[:].indirect(idx[:]))
         scatter((1, 2), FIRST_PIECES)
+        nc.vector.tensor_copy(out=v_words[:], in_=tab[:].indirect(idx[:]))
         lo, hi = CHUNKS[0]
         nc.scalar.copy(out=woven1[lo][:].rearrange("p (c t) -> p c t", t=PACK)[:, :, 2:4],
                        in_=planes[1, 2][:, lo:hi].unsqueeze(2).to_broadcast([P, hi - lo, 2]))

@@ -62,10 +62,13 @@ def tile_list_tidal_pitch_features_kernel(tc, tab_words, tab_scales, offs, offs2
         planes = {aj: sbuf([P, T], F32, "plane%d%d" % aj) for aj in ORDER}
         fresh = {aj: sbuf([P, S], F32, "fresh%d%d" % aj) for aj in ORDER}
 
-        def load_plane(aj, pieces=((0, S),)):
-            nc.sync.dma_start(out=planes[aj][:], in_=base_rows[aj[0], aj[1]])
+        def load_fresh(aj, pieces):
             for lo, hi in pieces:
                 nc.sync.dma_start(out=fresh[aj][:, lo:hi], in_=xs_rows[aj[0], aj[1]][:, lo:hi])
+
+        def load_plane(aj, pieces=((0, S),)):
+            nc.sync.dma_start(out=planes[aj][:], in_=base_rows[aj[0], aj[1]])
+            load_fresh(aj, pieces)
 
         def scatter(aj, pieces=((0, S),)):
             for lo, hi in pieces:
@@ -91,10 +94,11 @@ def tile_list_tidal_pitch_features_kernel(tc, tab_words, tab_scales, offs, offs2
         idx3 = lists.tile([P, S // GROUP], U16, name="idx3")
         tab_rows = sbuf([P, T], U8, "tab_rows")
         nc.gpsimd.memset(tab_rows[0 : P - SCALE_ROWS, :].bitcast(I32), 0)
-        nc.sync.dma_start(out=tab_rows[P - SCALE_ROWS : P, :].bitcast(I32), in_=tab_scales[0].bitcast(I32))
+        nc.scalar.dma_start(out=tab_rows[P - SCALE_ROWS : P, :].bitcast(I32), in_=tab_scales[0].bitcast(I32))
         nc.sync.dma_start(out=idx[:], in_=offs)
+        load_plane(ORDER[0], ())
         nc.sync.dma_start(out=idx2[:], in_=offs2)
-        load_plane(ORDER[0], FIRST_PIECES)
+        load_fresh(ORDER[0], FIRST_PIECES)
         tab = sbuf([P, T], U32, "tab")
         nc.sync.dma_start(out=tab[:].bitcast(I32), in_=tab_words[0].rearrange("p t i -> p (t i)").bitcast(I32))
 

@@ -29,7 +29,7 @@ HALF = T // 2
 AL = 64
 
 ORDER = [(1, 2), (0, 0), (0, 1), (0, 2), (0, 3), (1, 0), (1, 1), (1, 3)]
-FIRST_PIECES = ((0, S // 4), (S // 4, S))
+FIRST_PIECES = ((0, 3 * S // 8), (3 * S // 8, S))
 CHUNKS = [(1536, 2048), (0, 512), (512, 1024), (1024, 1280), (1280, 1536)]
 BANK_ORDER = [3, 0, 1, 2]
 GPSIMD_CHUNKS = 1
@@ -98,9 +98,10 @@ def tile_list_tidal_pitch_features_kernel(tc, tab_words, tab_scales, offs, offs2
         nc.sync.dma_start(out=idx[:], in_=offs)
         load_plane(ORDER[0], ())
         nc.sync.dma_start(out=idx2[:], in_=offs2)
-        load_fresh(ORDER[0], FIRST_PIECES)
+        load_fresh(ORDER[0], FIRST_PIECES[:1])
         tab = sbuf([P, T], U32, "tab")
         nc.sync.dma_start(out=tab[:].bitcast(I32), in_=tab_words[0].rearrange("p t i -> p (t i)").bitcast(I32))
+        load_fresh(ORDER[0], FIRST_PIECES[1:])
 
         wsc_raw = sbuf([P, 2 * H], U8, "wsc_raw")
         wsc_raw_scales = sbuf([P, H], U8, "wsc_raw_scales")
@@ -151,8 +152,9 @@ def tile_list_tidal_pitch_features_kernel(tc, tab_words, tab_scales, offs, offs2
         nc.gpsimd.memset(v_scales[:].bitcast(I32), 0)
         move_scale_rows(nc.scalar, v_scales, v_rows[P - SCALE_ROWS : P, :])
         v_words = sbuf([P, S], U32, "v_words")
-        scatter((1, 2), FIRST_PIECES)
+        scatter((1, 2), FIRST_PIECES[:1])
         nc.vector.tensor_copy(out=v_words[:], in_=tab[:].indirect(idx[:]))
+        scatter((1, 2), FIRST_PIECES[1:])
         lo, hi = CHUNKS[0]
         nc.scalar.copy(out=woven1[lo][:].rearrange("p (c t) -> p c t", t=PACK)[:, :, 2:4],
                        in_=planes[1, 2][:, lo:hi].unsqueeze(2).to_broadcast([P, hi - lo, 2]))

@@ -30,10 +30,11 @@ AL = 64
 
 ORDER = [(1, 2), (0, 0), (0, 1), (0, 2), (0, 3), (1, 0), (1, 1), (1, 3)]
 FIRST_PIECES = ((0, 3 * S // 8), (3 * S // 8, S))
-CHUNKS = [(1536, 2048), (0, 512), (512, 1024), (1024, 1280), (1280, 1536)]
-BANK_ORDER = [3, 0, 1, 2]
-GPSIMD_CHUNKS = 1
-VECTOR_WEAVES = 512
+CHUNKS = [(0, 512), (512, 1024), (1024, 1536), (1536, 1792), (1792, 2048)]
+WOVEN = [(0, 1024), (1024, 1536), (1536, 1792), (1792, 2048)]
+BANK_ORDER = [0, 1, 2, 3]
+GPSIMD_WEAVES = 256
+VECTOR_WEAVES = 480
 TURNED = 3
 PIECE = 2 * P
 
@@ -131,8 +132,10 @@ def tile_list_tidal_pitch_features_kernel(tc, tab_words, tab_scales, offs, offs2
 
         border = T * 4
         woven1 = {}
-        for lo, hi in CHUNKS[:-GPSIMD_CHUNKS]:
+        for lo, hi in WOVEN[:-2] + WOVEN[-1:]:
             woven1[lo] = sbuf([P, (hi - lo) * PACK], BF16, "woven1_%d" % lo)
+        lo, hi = WOVEN[-2]
+        woven1[lo] = placed.tile([P, (hi - lo) * PACK], BF16, name="woven1_%d" % lo, offset=border - (hi - lo) * PACK, align_bytes=AL)
 
         def weave_plane(engine_copy, j, lo, hi, first=None, last=None):
             first, last = first or lo, last or hi
@@ -141,7 +144,7 @@ def tile_list_tidal_pitch_features_kernel(tc, tab_words, tab_scales, offs, offs2
 
         ident = sbuf([P, P], F32, "ident")
         make_identity(nc, ident[:])
-        stage = placed.tile([P, PACK, T], BF16, name="stage", offset=border, align_bytes=AL)
+        stage = placed.tile([P, PACK, T], BF16, name="stage", offset=border + (6 * P + H) * 4, align_bytes=AL)
 
         def stage_plane(j):
             nc.scalar.copy(out=stage[:, j, :], in_=planes[0, j][:])
@@ -155,10 +158,10 @@ def tile_list_tidal_pitch_features_kernel(tc, tab_words, tab_scales, offs, offs2
         scatter((1, 2), FIRST_PIECES[:1])
         nc.vector.tensor_copy(out=v_words[:], in_=tab[:].indirect(idx[:]))
         scatter((1, 2), FIRST_PIECES[1:])
-        lo, hi = CHUNKS[0]
+        lo, hi = WOVEN[0]
         nc.scalar.copy(out=woven1[lo][:].rearrange("p (c t) -> p c t", t=PACK)[:, :, 2:4],
                        in_=planes[1, 2][:, lo:hi].unsqueeze(2).to_broadcast([P, hi - lo, 2]))
-        for lo, hi in CHUNKS[1:-GPSIMD_CHUNKS]:
+        for lo, hi in WOVEN[1:]:
             weave_plane(nc.scalar.copy, 2, lo, hi)
         wsc_sorted = sbuf([P, 3 * H], U8, "wsc_sorted")
         nc.gpsimd.tensor_copy(out=wsc_sorted[:, 0 : 2 * H].rearrange("p (t m b) -> p t m b", t=PACK, b=2),
@@ -192,18 +195,17 @@ def tile_list_tidal_pitch_features_kernel(tc, tab_words, tab_scales, offs, offs2
         for lo, hi in ((HALF, T - P), (0, HALF), (T - P, T)):
             gpsimd_copy(out=woven0[lo // HALF][:, lo % HALF * PACK : (lo % HALF + hi - lo) * PACK].rearrange("p (c t) -> p c t", t=PACK),
                         in_=stage[:, :, lo:hi].rearrange("p t c -> p c t"))
-        for (lo, hi), offset in zip(CHUNKS[-GPSIMD_CHUNKS:], (border - 2 * P * PACK,)):
-            woven1[lo] = placed.tile([P, (hi - lo) * PACK], BF16, name="woven1_%d" % lo, offset=offset, align_bytes=AL)
-            gpsimd_copy(out=woven1[lo][:].rearrange("p (c t) -> p c t", t=PACK)[:, :, 2:4],
-                        in_=planes[1, 2][:, lo:hi].unsqueeze(2).to_broadcast([P, hi - lo, 2]))
         for j in range(2):
             scatter((1, j))
-            for i, (lo, hi) in enumerate(CHUNKS):
-                weave_plane(nc.scalar.copy if i < len(CHUNKS) - GPSIMD_CHUNKS else gpsimd_copy, j, lo, hi)
+            for lo, hi in WOVEN:
+                weave_plane(nc.scalar.copy, j, lo, hi, max(lo, GPSIMD_WEAVES), hi)
+            slots = slice(j, PACK, PACK - 2 * j)
+            gpsimd_copy(out=woven1[0][:].rearrange("p (c t) -> p c t", t=PACK)[:, 0:GPSIMD_WEAVES, slots],
+                        in_=planes[1, j][:, 0:GPSIMD_WEAVES].unsqueeze(2).to_broadcast([P, GPSIMD_WEAVES, j + 1]))
         scatter((1, 3))
 
         page_scales = [sbuf([P, T], U8, "page_scales%d" % a) for a in range(2)]
-        early_codes = sbuf([P, T + 2 * P], U32, "early_codes", "fresh13")
+        early_codes = sbuf([P, T + 2 * P], U32, "early_codes", "plane10")
         page_codes = [early_codes[:, 0:T], sbuf([P, T], U32, "page_codes1", "wp0_raw")[:]]
         weight_scales = sbuf([P, 3 * H], U8, "weight_scales")
         weight_codes = {}
@@ -225,21 +227,23 @@ def tile_list_tidal_pitch_features_kernel(tc, tab_words, tab_scales, offs, offs2
                                 start=start, stop=stop)
 
         quantize_page(0, 0, HALF, woven0[0][:])
-        lo, hi = CHUNKS[0]
-        weave_plane(nc.vector.tensor_copy, 3, lo, hi, lo, lo + VECTOR_WEAVES)
-        for lo, hi in CHUNKS[1:]:
+        weave_plane(nc.vector.tensor_copy, 3, 0, HALF, 0, VECTOR_WEAVES)
+        weave_plane(nc.scalar.copy, 3, 0, HALF, VECTOR_WEAVES, HALF)
+        for lo, hi in WOVEN[1:]:
             weave_plane(nc.scalar.copy, 3, lo, hi)
-        quantize_page(0, HALF, T, woven0[1][:])
+        quantize_page(0, HALF, HALF + BANK, woven0[1][:, 0 : BANK * PACK])
         shares = [CHUNKS[0:1], CHUNKS[1:2], CHUNKS[2:3], CHUNKS[3:5]]
         first_accs = [bank(b, [P, share[-1][1] - share[0][0]], "acc0_%d" % b) for b, share in enumerate(shares)]
-        upper_half_first = sorted(zip(first_accs, shares), key=lambda pair: pair[1][0][0] >= HALF)
-        for acc, share in upper_half_first:
-            for lo, hi in share:
-                page_pass(acc[:, lo - share[0][0] : hi - share[0][0]], 0, 0, lo, hi, lo == share[0][0], False)
+        for acc, share in zip(first_accs[:-1], shares):
+            page_pass(acc[:], 0, 0, share[0][0], share[0][1], True, False)
         for acc, share in zip(first_accs, shares):
             for lo, hi in share:
-                quantize_page(1, lo, hi, woven1[lo][:])
+                first = max(start for start, end in WOVEN if start <= lo)
+                quantize_page(1, lo, hi, woven1[first][:, (lo - first) * PACK : (hi - first) * PACK])
                 page_pass(acc[:, lo - share[0][0] : hi - share[0][0]], 0, 1, lo, hi, False, hi == share[-1][1])
+            if share == shares[0]:
+                quantize_page(0, HALF + BANK, T, woven0[1][:, BANK * PACK : HALF * PACK])
+                page_pass(first_accs[-1][:], 0, 0, HALF + BANK, T, True, False)
         late_codes = placed.tile([P, 6 * P + H], U32, name="late_codes", offset=border, align_bytes=AL)
         quantize_weights(late_codes[:, 0 : 2 * P], 2, 4)
         proj = [sbuf([P, T], F32, "proj0", "plane00")]

@@ -34,7 +34,7 @@ CHUNKS = [(0, 512), (512, 1024), (1024, 1536), (1536, 1792), (1792, 2048)]
 WOVEN = [(0, 1024), (1024, 1536), (1536, 1792), (1792, 2048)]
 BANK_ORDER = [0, 1, 2, 3]
 GPSIMD_WEAVES = 256
-VECTOR_WEAVES = 480
+VECTOR_WEAVES = 576
 TURNED = 3
 PIECE = 2 * P
 

@@ -35,6 +35,7 @@ WOVEN = [(0, 1024), (1024, 1536), (1536, 1792), (1792, 2048)]
 BANK_ORDER = [0, 1, 2, 3]
 GPSIMD_WEAVES = 256
 VECTOR_WEAVES = 576
+PAIRED = [(0, 2), (1, 0)]
 TURNED = 3
 PIECE = 2 * P
 
@@ -61,7 +62,11 @@ def tile_list_tidal_pitch_features_kernel(tc, tab_words, tab_scales, offs, offs2
         base_rows = base.rearrange("(a p j) t -> a j p t", p=P, j=PACK)
         xs_rows = xs.rearrange("(a p j) t -> a j p t", p=P, j=PACK)
         planes = {aj: sbuf([P, T], F32, "plane%d%d" % aj) for aj in ORDER}
-        fresh = {aj: sbuf([P, S], F32, "fresh%d%d" % aj) for aj in ORDER}
+        fresh = {aj: sbuf([P, S], F32, "fresh%d%d" % aj)[:] for aj in ORDER if aj not in PAIRED and (aj[0], aj[1] - 1) not in PAIRED}
+        fresh_pairs = {aj: sbuf([P, 2, S], F32, "fresh%d%d" % aj) for aj in PAIRED}
+        for a, j in PAIRED:
+            for i in range(2):
+                fresh[a, j + i] = fresh_pairs[a, j][:, i, :]
 
         def load_fresh(aj, pieces):
             for lo, hi in pieces:
@@ -69,7 +74,11 @@ def tile_list_tidal_pitch_features_kernel(tc, tab_words, tab_scales, offs, offs2
 
         def load_plane(aj, pieces=((0, S),)):
             nc.sync.dma_start(out=planes[aj][:], in_=base_rows[aj[0], aj[1]])
-            load_fresh(aj, pieces)
+            if aj in PAIRED:
+                nc.sync.dma_start(out=fresh_pairs[aj][:],
+                                  in_=xs.rearrange("(a p j) t -> a p j t", p=P, j=PACK)[aj[0]][:, aj[1] : aj[1] + 2, :])
+            elif (aj[0], aj[1] - 1) not in PAIRED:
+                load_fresh(aj, pieces)
 
         def scatter(aj, pieces=((0, S),)):
             for lo, hi in pieces:
@@ -350,10 +359,12 @@ def tile_list_tidal_pitch_features_kernel(tc, tab_words, tab_scales, offs, offs2
                     nc.vector.tensor_scalar(out=result[:, h, :], in0=y[:], scalar1=bo_cols[:, h : h + 1], scalar2=None, op0=ALU.add)
                 else:
                     nc.scalar.activation(out=result[:, h, :], in_=y[:], func=ACT.Identity, bias=bo_cols[:, h : h + 1])
+                if first < last:
+                    nc.sync.dma_start(out=out_rows[:, h, cols], in_=result[:, h, :])
             if hi == S:
                 nc.scalar.dma_start(out=out_rows[:, 0, cols], in_=result[:, 0, :])
                 nc.sync.dma_start(out=out_rows[:, 1, cols], in_=result[:, 1, :])
-            else:
+            elif first == last:
                 nc.sync.dma_start(out=out_rows[:, :, cols], in_=result[:])
 
         couple(0)

from contextlib import ExitStack

import concourse.mybir as mybir
from concourse.masks import make_identity

F32 = mybir.dt.float32
BF16 = mybir.dt.bfloat16
I32 = mybir.dt.int32
U32 = mybir.dt.uint32
U16 = mybir.dt.uint16
U8 = mybir.dt.uint8
FP8X4 = mybir.dt.float8_e4m3fn_x4
FP4X4 = mybir.dt.float4_e2m1fn_x4
ACT = mybir.ActivationFunctionType
ALU = mybir.AluOpType

FLOPS = 3489660928

P = 128
PACK = 4
T = 2048
S = 1024
H = 512
N = 256
GROUP = 16
SCALE_ROWS = 16
BANK = 512
HALF = T // 2
AL = 64

ORDER = [(1, 2), (0, 0), (0, 1), (0, 2), (0, 3), (1, 0), (1, 1), (1, 3)]
FIRST_PIECES = ((0, 3 * S // 8), (3 * S // 8, S))
CHUNKS = [(0, 512), (512, 1024), (1024, 1536), (1536, 1792), (1792, 2048)]
WOVEN = [(0, 1024), (1024, 1536), (1536, 1792), (1792, 2048)]
BANK_ORDER = [0, 1, 2, 3]
GPSIMD_WEAVES = 256
VECTOR_WEAVES = 576
PAIRED = [(0, 2), (1, 0)]
TURNED = 3
PIECE = 2 * P


def tile_list_tidal_pitch_features_kernel(tc, tab_words, tab_scales, offs, offs2, offs3, xs, base, wp,
                                                    wsc_words, wsc_scales, wsh, amp, wo_words, wo_scales, bo, out):
    nc = tc.nc
    with ExitStack() as ctx:
        lists = ctx.enter_context(tc.tile_pool(name="lists", bufs=1))
        sb = ctx.enter_context(tc.tile_pool(name="sb", bufs=1))
        psum = ctx.enter_context(tc.psum_pool(name="psum", bufs=1))
        placed = ctx.enter_context(tc.tile_pool(name="placed", bufs=1))

        def sbuf(shape, dtype, name, tag=None):
            return sb.tile(shape, dtype, name=name, tag=tag or name, align_bytes=AL)

        def bank(b, shape, name):
            return psum.tile(shape, F32, name=name, tag="bank%d" % b)

        def move_scale_rows(queue, scales, rows):
            for q in range(4):
                queue.dma_start(out=scales[32 * q : 32 * q + 4, :].bitcast(I32), in_=rows[4 * q : 4 * q + 4, :].bitcast(I32))

        base_rows = base.rearrange("(a p j) t -> a j p t", p=P, j=PACK)
        xs_rows = xs.rearrange("(a p j) t -> a j p t", p=P, j=PACK)
        planes = {aj: sbuf([P, T], F32, "plane%d%d" % aj) for aj in ORDER}
        fresh = {aj: sbuf([P, S], F32, "fresh%d%d" % aj)[:] for aj in ORDER if aj not in PAIRED and (aj[0], aj[1] - 1) not in PAIRED}
        fresh_pairs = {aj: sbuf([P, 2, S], F32, "fresh%d%d" % aj) for aj in PAIRED}
        for a, j in PAIRED:
            for i in range(2):
                fresh[a, j + i] = fresh_pairs[a, j][:, i, :]

        def load_fresh(aj, pieces):
            for lo, hi in pieces:
                nc.sync.dma_start(out=fresh[aj][:, lo:hi], in_=xs_rows[aj[0], aj[1]][:, lo:hi])

        def load_plane(aj, pieces=((0, S),)):
            nc.sync.dma_start(out=planes[aj][:], in_=base_rows[aj[0], aj[1]])
            if aj in PAIRED:
                nc.sync.dma_start(out=fresh_pairs[aj][:],
                                  in_=xs.rearrange("(a p j) t -> a p j t", p=P, j=PACK)[aj[0]][:, aj[1] : aj[1] + 2, :])
            elif (aj[0], aj[1] - 1) not in PAIRED:
                load_fresh(aj, pieces)

        def scatter(aj, pieces=((0, S),)):
            for lo, hi in pieces:
                nc.vector.tensor_copy(out=planes[aj][:].indirect(idx2[:, lo // GROUP : hi // GROUP]), in_=fresh[aj][:, lo:hi])

        def load_weight(rows, name):
            raw = sbuf([P, PACK, H], F32, name)
            nc.sync.dma_start(out=raw[:], in_=rows.rearrange("(p j) r -> p j r", j=PACK))
            return raw

        def gpsimd_copy(out, in_):
            nc.gpsimd.tensor_scalar(out=out, in0=in_, scalar1=1.0, scalar2=0.0, op0=ALU.mult, op1=ALU.add)

        def weave_weight(engine_copy, raw, woven, walk):
            engine_copy(out=woven.rearrange("p t (m j) -> " + walk, j=PACK),
                        in_=raw[:].rearrange("p j (m t) -> " + walk, t=PACK))

        def quantize(codes, scales, woven):
            nc.vector.quantize_mx(out=codes.bitcast(FP8X4), scales=scales, in_=woven)

        idx = lists.tile([P, S // GROUP], U16, name="idx")
        idx2 = lists.tile([P, S // GROUP], U16, name="idx2")
        idx3 = lists.tile([P, S // GROUP], U16, name="idx3")
        tab_rows = sbuf([P, T], U8, "tab_rows")
        nc.gpsimd.memset(tab_rows[0 : P - SCALE_ROWS, :].bitcast(I32), 0)
        nc.scalar.dma_start(out=tab_rows[P - SCALE_ROWS : P, :].bitcast(I32), in_=tab_scales[0].bitcast(I32))
        nc.sync.dma_start(out=idx[:], in_=offs)
        load_plane(ORDER[0], ())
        nc.sync.dma_start(out=idx2[:], in_=offs2)
        load_fresh(ORDER[0], FIRST_PIECES[:1])
        tab = sbuf([P, T], U32, "tab")
        nc.sync.dma_start(out=tab[:].bitcast(I32), in_=tab_words[0].rearrange("p t i -> p (t i)").bitcast(I32))
        load_fresh(ORDER[0], FIRST_PIECES[1:])

        wsc_raw = sbuf([P, 2 * H], U8, "wsc_raw")
        wsc_raw_scales = sbuf([P, H], U8, "wsc_raw_scales")
        wo_block_scales = sbuf([P, N], U8, "wo_block_scales")
        amp_cols = sbuf([P, PACK], F32, "amp_cols")
        nc.gpsimd.memset(wsc_raw_scales[:].bitcast(I32), 0)
        nc.gpsimd.memset(wo_block_scales[:].bitcast(I32), 0)

        load_plane(ORDER[1])
        nc.sync.dma_start(out=wsc_raw[:].bitcast(I32), in_=wsc_words[0].bitcast(I32))
        move_scale_rows(nc.sync, wsc_raw_scales, wsc_scales[0])
        nc.sync.dma_start(out=amp_cols[:], in_=amp.rearrange("(p t) -> p t", t=PACK))
        wp_raw = [load_weight(wp[0:H, :], "wp0_raw")]
        load_plane(ORDER[2])
        wp_raw.append(load_weight(wp[H : 2 * H, :], "wp1_raw"))
        load_plane(ORDER[3])
        wsh_raw = load_weight(wsh, "wsh_raw")
        for aj in ORDER[4:]:
            load_plane(aj)
        nc.sync.dma_start(out=idx3[:], in_=offs3)
        wo_codes = sbuf([P, N], U32, "wo_codes")
        nc.sync.dma_start(out=wo_codes[:].bitcast(I32), in_=wo_words[0].rearrange("p c i -> p (c i)").bitcast(I32))
        move_scale_rows(nc.sync, wo_block_scales, wo_scales[0])
        bo_cols = sbuf([P, 2], F32, "bo_cols")
        with nc.allow_non_contiguous_dma(reason="one bias value a partition"):
            nc.sync.dma_start(out=bo_cols[:], in_=bo.rearrange("(h p) -> p h", p=P))

        border = T * 4
        woven1 = {}
        for lo, hi in WOVEN[:-2] + WOVEN[-1:]:
            woven1[lo] = sbuf([P, (hi - lo) * PACK], BF16, "woven1_%d" % lo)
        lo, hi = WOVEN[-2]
        woven1[lo] = placed.tile([P, (hi - lo) * PACK], BF16, name="woven1_%d" % lo, offset=border - (hi - lo) * PACK, align_bytes=AL)

        def weave_plane(engine_copy, j, lo, hi, first=None, last=None):
            first, last = first or lo, last or hi
            engine_copy(out=woven1[lo][:].rearrange("p (c t) -> p c t", t=PACK)[:, first - lo : last - lo, j],
                        in_=planes[1, j][:, first:last])

        ident = sbuf([P, P], F32, "ident")
        make_identity(nc, ident[:])
        stage = placed.tile([P, PACK, T], BF16, name="stage", offset=border + (6 * P + H) * 4, align_bytes=AL)

        def stage_plane(j):
            nc.scalar.copy(out=stage[:, j, :], in_=planes[0, j][:])

        v_rows = sbuf([P, S], U8, "v_rows")
        nc.vector.tensor_copy(out=v_rows[:], in_=tab_rows[:].indirect(idx[:]))
        v_scales = sbuf([P, S], U8, "v_scales")
        nc.gpsimd.memset(v_scales[:].bitcast(I32), 0)
        move_scale_rows(nc.scalar, v_scales, v_rows[P - SCALE_ROWS : P, :])
        v_words = sbuf([P, S], U32, "v_words")
        scatter((1, 2), FIRST_PIECES[:1])
        nc.vector.tensor_copy(out=v_words[:], in_=tab[:].indirect(idx[:]))
        scatter((1, 2), FIRST_PIECES[1:])
        lo, hi = WOVEN[0]
        nc.scalar.copy(out=woven1[lo][:].rearrange("p (c t) -> p c t", t=PACK)[:, :, 2:4],
                       in_=planes[1, 2][:, lo:hi].unsqueeze(2).to_broadcast([P, hi - lo, 2]))
        for lo, hi in WOVEN[1:]:
            weave_plane(nc.scalar.copy, 2, lo, hi)
        wsc_sorted = sbuf([P, 3 * H], U8, "wsc_sorted")
        nc.gpsimd.tensor_copy(out=wsc_sorted[:, 0 : 2 * H].rearrange("p (t m b) -> p t m b", t=PACK, b=2),
                              in_=wsc_raw[:].rearrange("p (m t b) -> p t m b", t=PACK, b=2))
        nc.gpsimd.tensor_copy(out=wsc_sorted[:, 2 * H : 3 * H].rearrange("p (t m) -> p t m", t=PACK),
                              in_=wsc_raw_scales[:].rearrange("p (m t) -> p t m", t=PACK))
        scatter((0, 0))
        stage_plane(0)
        weights = sbuf([P, 3 * PACK, P * PACK], BF16, "weights")
        wp_woven = weights[:, 0 : 2 * PACK, :].rearrange("p (t a) c -> p t a c", a=2)
        weave_weight(nc.scalar.copy, wp_raw[0], wp_woven[:, :, 0, :], "p m j t")
        gain = sbuf([P, PACK, S], F32, "gain")
        for t in range(PACK):
            for h in range(S // BANK):
                cols = slice(h * BANK, (h + 1) * BANK)
                sc = bank(2 * t + h, [P, BANK], "sc%d_%d" % (t, h))
                nc.tensor.matmul_mx(out=sc[:], lhsT=wsc_sorted[:, 2 * P * t : 2 * P * (t + 1)].bitcast(FP4X4),
                                    lhsT_scale=wsc_sorted[:, 2 * H + P * t : 2 * H + P * (t + 1)],
                                    rhs=v_words[:, cols].bitcast(FP8X4), rhs_scale=v_scales[:, cols],
                                    start=True, stop=True)
                nc.scalar.activation(out=gain[:, t, cols], in_=sc[:], func=ACT.Exp, scale=amp_cols[:, t : t + 1])
        scatter((0, 1))
        stage_plane(1)
        weave_weight(nc.scalar.copy, wp_raw[1], wp_woven[:, :, 1, :], "p m j t")
        scatter((0, 2))
        stage_plane(2)
        weave_weight(nc.scalar.copy, wsh_raw, weights[:, 2 * PACK : 3 * PACK, :], "p m j t")
        scatter((0, 3))
        stage_plane(3)
        woven0 = [sbuf([P, HALF * PACK], BF16, "woven0_%d" % h, "wp%d_raw" % h) for h in range(2)]
        for lo, hi in ((HALF, T - P), (0, HALF), (T - P, T)):
            gpsimd_copy(out=woven0[lo // HALF][:, lo % HALF * PACK : (lo % HALF + hi - lo) * PACK].rearrange("p (c t) -> p c t", t=PACK),
                        in_=stage[:, :, lo:hi].rearrange("p t c -> p c t"))
        for j in range(2):
            scatter((1, j))
            for lo, hi in WOVEN:
                weave_plane(nc.scalar.copy, j, lo, hi, max(lo, GPSIMD_WEAVES), hi)
            slots = slice(j, PACK, PACK - 2 * j)
            gpsimd_copy(out=woven1[0][:].rearrange("p (c t) -> p c t", t=PACK)[:, 0:GPSIMD_WEAVES, slots],
                        in_=planes[1, j][:, 0:GPSIMD_WEAVES].unsqueeze(2).to_broadcast([P, GPSIMD_WEAVES, j + 1]))
        scatter((1, 3))

        page_scales = [sbuf([P, T], U8, "page_scales%d" % a) for a in range(2)]
        early_codes = sbuf([P, T + 2 * P], U32, "early_codes", "plane10")
        page_codes = [early_codes[:, 0:T], sbuf([P, T], U32, "page_codes1", "wp0_raw")[:]]
        weight_scales = sbuf([P, 3 * H], U8, "weight_scales")
        weight_codes = {}

        def quantize_weights(codes, first, last):
            quantize(codes, weight_scales[:, first * P : last * P], weights[:, first:last, :].rearrange("p b c -> p (b c)"))
            for b in range(first, last):
                weight_codes[b] = codes[:, (b - first) * P : (b - first + 1) * P]

        quantize_weights(early_codes[:, T : T + 2 * P], 0, 2)

        def quantize_page(a, lo, hi, woven):
            quantize(page_codes[a][:, lo:hi], page_scales[a][:, lo:hi], woven)

        def page_pass(acc, t, a, lo, hi, start, stop):
            nc.tensor.matmul_mx(out=acc, lhsT=weight_codes[2 * t + a].bitcast(FP8X4),
                                lhsT_scale=weight_scales[:, P * (2 * t + a) : P * (2 * t + a + 1)],
                                rhs=page_codes[a][:, lo:hi].bitcast(FP8X4), rhs_scale=page_scales[a][:, lo:hi],
                                start=start, stop=stop)

        quantize_page(0, 0, HALF, woven0[0][:])
        weave_plane(nc.vector.tensor_copy, 3, 0, HALF, 0, VECTOR_WEAVES)
        weave_plane(nc.scalar.copy, 3, 0, HALF, VECTOR_WEAVES, HALF)
        for lo, hi in WOVEN[1:]:
            weave_plane(nc.scalar.copy, 3, lo, hi)
        quantize_page(0, HALF, HALF + BANK, woven0[1][:, 0 : BANK * PACK])
        shares = [CHUNKS[0:1], CHUNKS[1:2], CHUNKS[2:3], CHUNKS[3:5]]
        first_accs = [bank(b, [P, share[-1][1] - share[0][0]], "acc0_%d" % b) for b, share in enumerate(shares)]
        for acc, share in zip(first_accs[:-1], shares):
            page_pass(acc[:], 0, 0, share[0][0], share[0][1], True, False)
        for acc, share in zip(first_accs, shares):
            for lo, hi in share:
                first = max(start for start, end in WOVEN if start <= lo)
                quantize_page(1, lo, hi, woven1[first][:, (lo - first) * PACK : (hi - first) * PACK])
                page_pass(acc[:, lo - share[0][0] : hi - share[0][0]], 0, 1, lo, hi, False, hi == share[-1][1])
            if share == shares[0]:
                quantize_page(0, HALF + BANK, T, woven0[1][:, BANK * PACK : HALF * PACK])
                page_pass(first_accs[-1][:], 0, 0, HALF + BANK, T, True, False)
        late_codes = placed.tile([P, 6 * P + H], U32, name="late_codes", offset=border, align_bytes=AL)
        quantize_weights(late_codes[:, 0 : 2 * P], 2, 4)
        proj = [sbuf([P, T], F32, "proj0", "plane00")]
        for acc, share in zip(first_accs, shares):
            nc.scalar.copy(out=proj[0][:, share[0][0] : share[-1][1]], in_=acc[:])
        quantize_weights(late_codes[:, 2 * P : 10 * P], 4, 12)
        for t in range(1, PACK):
            if t == 1:
                proj.append(placed.tile([P, T], F32, name="proj1", offset=0, align_bytes=AL))
            else:
                proj.append(sbuf([P, T], F32, "proj%d" % t, "plane0%d" % t))
            for i, c in enumerate(BANK_ORDER):
                acc = bank(4 * (t % 2) + i, [P, BANK], "acc%d_%d" % (t, c))
                for a in range(2):
                    page_pass(acc[:], t, a, c * BANK, (c + 1) * BANK, a == 0, a == 1)
                nc.scalar.copy(out=proj[t][:, c * BANK : (c + 1) * BANK], in_=acc[:])

        scaled = placed.tile([P, PACK, S], F32, name="scaled", offset=border + (6 * P + H) * 4, align_bytes=AL)

        def gather(t, lo, hi):
            nc.vector.tensor_tensor(out=scaled[:, t, lo:hi], in0=proj[t][:].indirect(idx3[:, lo // GROUP : hi // GROUP]),
                                    in1=gain[:, t, lo:hi], op=ALU.mult)

        for t in range(PACK - 1):
            gather(t, 0, S)
        gather(PACK - 1, 0, 2 * P)
        gather(PACK - 1, 2 * P, 5 * P)
        z_codes = sbuf([P, S], U32, "z_codes", "fresh00")
        z_scales = sbuf([P, S], U8, "z_scales")
        out_rows = out.rearrange("(h p) j -> p h j", p=P)

        def shift(c, b):
            sh = bank(b, [P, PACK, P], "sh%d" % c)
            cols = slice(c * P, (c + 1) * P)
            for t in range(PACK):
                nc.tensor.matmul_mx(out=sh[:, t, :], lhsT=weight_codes[8 + t].bitcast(FP8X4),
                                    lhsT_scale=weight_scales[:, P * (8 + t) : P * (9 + t)],
                                    rhs=v_words[:, cols].bitcast(FP8X4), rhs_scale=v_scales[:, cols],
                                    start=True, stop=True)
            return sh

        shifts = {c: shift(c, b) for c, b in ((0, 0), (2, 1), (1, 2), (3, 3), (4, 4))}
        shift_sbuf = sbuf([P, TURNED, PACK, P], F32, "shift_sbuf", "plane12")
        pair_banks = [bank(5 + u, [P, 2, 2, P], "turned%d" % u) for u in range(2)]
        third_bank = bank(7, [P, PACK, P], "turned2")

        def turn(c, t, src, start, stop):
            acc = pair_banks[t // 2][:, c, t % 2, :] if c < 2 else third_bank[:, t, :]
            nc.tensor.matmul(out=acc, lhsT=src, rhs=ident[:], is_transpose=True, start=start, stop=stop)

        opens_a_bank = ((0, 0), (0, 2), (2, 0))
        for t in range(PACK - 1):
            for c in range(TURNED):
                turn(c, t, scaled[:, t, (2 + c) * P : (3 + c) * P], (c, t) in opens_a_bank, False)
        for c in range(TURNED):
            nc.scalar.copy(out=shift_sbuf[:, c, :, :], in_=shifts[2 + c][:])
        for c, t in [(c, t) for t in range(PACK) for c in range(2)] + [(2, t) for t in range(PACK)]:
            turn(c, t, shift_sbuf[:, c, t, :], False, (c, t) == (1, 1))
        for c in range(TURNED):
            turn(c, PACK - 1, scaled[:, PACK - 1, (2 + c) * P : (3 + c) * P], False, c > 0)
        for c, b in ((5, 1), (6, 3), (7, 4)):
            shifts[c] = shift(c, b)
        pairs = sbuf([P, TURNED, 2, 2 * P], BF16, "pairs", "fresh10")
        for u in range(2):
            nc.scalar.copy(out=pairs[:, 0:2, u, :].rearrange("j c (p e) -> j c p e", e=2),
                           in_=pair_banks[u][:].rearrange("j c e p -> j c p e"))
        nc.scalar.copy(out=pairs[:, 2, :, :].rearrange("j u (p e) -> j u p e", e=2),
                       in_=third_bank[:].rearrange("j (u e) p -> j u p e", e=2))
        z_bytes = PIECE * PACK * 2
        z_tiles = [sbuf([P, PIECE * PACK], BF16, "z0", "tab"),
                   placed.tile([P, PIECE * PACK], BF16, name="z1", offset=0, align_bytes=AL),
                   sbuf([P, PIECE * PACK], BF16, "z2", "fresh01")]

        def z_cols(lo, hi):
            return z_tiles[lo // PIECE][:, lo % PIECE * PACK : (lo % PIECE + hi - lo) * PACK]

        for c in range(TURNED):
            words = bank(5 + c, [P, 2, P], "words%d" % c)
            for u in range(2):
                nc.tensor.transpose(words[:, u, :], pairs[:, c, u, :].bitcast(F32), ident[:])
            nc.scalar.copy(out=z_cols((2 + c) * P, (3 + c) * P).bitcast(F32).rearrange("p (j u) -> p j u", u=2),
                           in_=words[:].rearrange("p u j -> p j u"))
        z_tiles.append(placed.tile([P, PIECE * PACK], BF16, name="z3", offset=z_bytes // 2, align_bytes=AL))

        def couple(c):
            nc.vector.tensor_tensor(
                out=z_cols(c * P, (c + 1) * P).rearrange("p (c i t) -> p c t i", i=2, t=PACK),
                in0=scaled[:, :, c * P : (c + 1) * P].rearrange("p t (c i) -> p c t i", i=2),
                in1=shifts[c][:].rearrange("p t (c i) -> p c t i", i=2), op=ALU.add)

        def finish(first, last, banks, tag):
            lo, hi = first * P, (last + 1) * P
            cols = slice(lo, hi)
            codes = z_codes[:, cols]
            quantize(codes, z_scales[:, cols], z_cols(lo, hi))
            result = sbuf([P, 2, hi - lo], F32, "result%d" % lo, tag)
            for h in range(N // P):
                y = bank(banks[h], [P, hi - lo], "y%d_%d" % (lo, h))
                nc.tensor.matmul_mx(out=y[:], lhsT=wo_codes[:, P * h : P * (h + 1)].bitcast(FP8X4),
                                    lhsT_scale=wo_block_scales[:, P * h : P * (h + 1)],
                                    rhs=codes.bitcast(FP8X4), rhs_scale=z_scales[:, cols],
                                    start=True, stop=True)
                if first == last and h == 1:
                    nc.vector.tensor_scalar(out=result[:, h, :], in0=y[:], scalar1=bo_cols[:, h : h + 1], scalar2=None, op0=ALU.add)
                else:
                    nc.scalar.activation(out=result[:, h, :], in_=y[:], func=ACT.Identity, bias=bo_cols[:, h : h + 1])
                if first < last:
                    nc.sync.dma_start(out=out_rows[:, h, cols], in_=result[:, h, :])
            if hi == S:
                nc.scalar.dma_start(out=out_rows[:, 0, cols], in_=result[:, 0, :])
                nc.sync.dma_start(out=out_rows[:, 1, cols], in_=result[:, 1, :])
            elif first == last:
                nc.sync.dma_start(out=out_rows[:, :, cols], in_=result[:])

        couple(0)
        couple(1)
        gather(PACK - 1, 5 * P, S)
        finish(0, 1, (0, 2), "weights")
        couple(5)
        finish(2, 3, (5, 6), "wsh_raw")
        finish(4, 5, (7, 1), "plane11")
        couple(6)
        couple(7)
        finish(6, 6, (3, 0), "plane10")
        finish(7, 7, (4, 2), "gain")
